import numpy as np, ml_dtypes
CORES = [6,15,38,47]
N = 4
BF = ml_dtypes.bfloat16
S, D, H, CAP = 4096, 3, 64, 2048
def heads(x):
    return x.astype(np.float32).reshape(N, 8, 16, S)
def scores(z, v, t):
    return np.einsum("rgcs,rgc->rgs", z, v[:, :, t].astype(np.float32).reshape(N, 8, 16))
def layer(z, kept, w, gap, t):
    out = z.copy()
    for g in range(8):
        q = np.concatenate([z[r, g][:, kept[r][g]] for r in range(N)], axis=1)
        q = np.pad(q, ((0, 0), (H, H))); a = H
        for r in range(N):
            k = kept[r][g].size; d = int(gap[r, 16 * g, t])
            m = w[r, 16 * g:16 * g + 16, 48 * t:48 * t + 48].astype(np.float32)
            s = m[:, :16].T @ q[:, a:a + k] + m[:, 16:32].T @ q[:, a - d:a - d + k] + m[:, 32:].T @ q[:, a + d:a + d + k]
            out[r, g][:, kept[r][g]] = np.clip(np.rint(s * np.float32(0.125)), -15, 15)
            a += k
    return out
def run(x, v, w, th, gap):
    z = heads(x); kept = [[np.arange(S)] * 8 for r in range(N)]; cnt = np.zeros((D, N, 8), np.int64)
    for t in range(D):
        s = scores(z, v, t)
        kept = [[kept[r][g][s[r, g, kept[r][g]] >= th[r, 16 * g, t]] for g in range(8)] for r in range(N)]
        for r in range(N):
            for g in range(8): cnt[t, r, g] = kept[r][g].size
        z = layer(z, kept, w, gap, t)
    return z, cnt
def rows16(a):
    return np.repeat(a, 16, axis=1).astype(np.int32)
def shares(rng):
    k = [rng.integers(CAP // 2, CAP * 7 // 8 + 1, (N, 8))]
    for t in range(1, D): k.append(np.maximum(k[-1] * rng.integers(60, 91, (N, 8)) // 100, H))
    return np.stack(k)
def settle(d, want):
    x, v, w, gap = d["x"], d["v"], d["w"], d["gap"]
    z = heads(x); kept = [[np.arange(S)] * 8 for r in range(N)]; th = np.zeros((N, 8, D), np.int32)
    for t in range(D):
        s = scores(z, v, t)
        for r in range(N):
            for g in range(8):
                a = s[r, g, kept[r][g]]; e = np.sort(a)[::-1]; lim = int(e[min(int(want[t, r, g]), e.size) - 1])
                if np.count_nonzero(a >= lim) > CAP: lim += 1
                th[r, g, t] = lim; kept[r][g] = kept[r][g][a >= lim]
        z = layer(z, kept, w, gap, t)
    d["th"] = rows16(th); return d
def setup_inputs(rng):
    d = {"x": rng.integers(-15, 16, (N, 128, S)).astype(np.float32).astype(BF), "v": rng.integers(-7, 8, (N, 128, D)).astype(np.float32).astype(BF),
         "w": (2 * rng.integers(0, 2, (N, 128, 48 * D)) - 1).astype(np.float32).astype(BF), "th": None, "gap": rows16(rng.integers(1, H + 1, (N, 8, D)))}
    return settle(d, shares(rng))
def setup_inputs_caps(rng):
    d = setup_inputs(rng); x = d["x"]; s = scores(heads(x), d["v"], 0); g8 = np.arange(8)
    big = (np.arange(N)[:, None] + g8 + rng.integers(0, 2)) % 2 == 0
    for r in range(N):
        for g in range(8):
            k = CAP if big[r, g] else H; u = s[r, g]; o = np.argsort(-u, kind="stable"); late = o[k:]; late = late[u[late] == u[o[k - 1]]]
            b = x[r, 16 * g:16 * g + 16]; b[:, late] = b[:, o[-1:]]
    want = np.stack([np.where(big, CAP, H)] + [np.where(big & (g8 % 4 < 2), CAP, H)] * (D - 1))
    d["gap"] = rows16(rng.choice(np.array([1, H]), (N, 8, D))); return settle(d, want)
def setup_inputs_ends(rng):
    d = setup_inputs(rng); x = d["x"]; s = scores(heads(x), d["v"], 0); k = int(rng.integers(0, 3))
    for r in range(N):
        for g in range(8):
            o = np.argsort(-s[r, g], kind="stable"); m = (r + g + k) % 3
            if m == 1: o = o[::-1]
            if m == 2: o = np.concatenate([o[0::2], o[1::2][::-1]])
            x[r, 16 * g:16 * g + 16] = x[r, 16 * g:16 * g + 16][:, o]
    d["gap"] = rows16(rng.choice(np.array([1, H]), (N, 8, D))); return settle(d, shares(rng))
def setup_inputs_ties(rng):
    d = setup_inputs(rng); c = rng.integers(0, 16, (N, 8, 1, D)); sg = 2 * rng.integers(0, 2, (N, 8, 1, D)) - 1
    d["v"] = ((np.arange(16)[:, None] == c) * sg).reshape(N, 128, D).astype(np.float32).astype(BF)
    return settle(d, shares(rng))
def setup_inputs_spread(rng):
    d = setup_inputs(rng); m = rng.integers(0, 16, (N, 8, 1, S))
    d["x"] = np.rint((2 * rng.random((N, 8, 16, S)) - 1) * m).reshape(N, 128, S).astype(np.float32).astype(BF)
    return settle(d, shares(rng))
def check_inputs(d):
    bad = []; x, v, w = [np.asarray(d[k]).astype(np.float32) for k in ("x", "v", "w")]; th, gap = d["th"], d["gap"]
    if not ((np.rint(x) == x) & (np.abs(x) <= 15)).all(): bad.append("x_whole_within_15")
    if not ((np.rint(v) == v) & (np.abs(v) <= 7)).all(): bad.append("v_whole_within_7")
    if not (np.abs(w) == 1).all(): bad.append("w_one_or_minus_one")
    a = th.reshape(N, 8, 16, D); b = gap.reshape(N, 8, 16, D)
    if (a != a[:, :, :1]).any() or (th < -4096).any() or (th > 4096).any(): bad.append("th")
    if (b != b[:, :, :1]).any() or (gap < 1).any() or (gap > H).any(): bad.append("gap")
    if bad: return bad
    cnt = run(x, v, w, th, gap)[1]
    if cnt.min() < H or cnt.max() > CAP: bad.append("numbers_kept")
    return bad
def reference(x, v, w, th, gap):
    z, cnt = run(x, v, w, th, gap)
    return {"y": z.reshape(N, 128, S).astype(np.float32)}

@@ -1,0 +1,430 @@
+from concourse.bass import DstId, RemoteDMATransfer
+from concourse.mybir import AluOpType, ActivationFunctionType
+
+OP = AluOpType
+AF = ActivationFunctionType
+CAP, HALO, OFS = 2048, 64, 192.0
+XW = HALO + CAP + HALO
+V1, Z1, V2, Z2, Z3, BIGW = 4096, 6144, 8192, 10240, 12288, 14336
+DWW, RMW = CAP + 256, 544
+
+_W = {"bfloat16": {"big": BIGW, "gb": CAP, "gc": CAP, "zr": CAP, "u": CAP, "cb": CAP, "dc": CAP, "dsb": 256, "mrow": 256,
+                   "e": 144, "bd": 128, "idn": 128, "idk": 128, "ltf": 128, "lt": 128, "s15": 128, "el1": 144, "el2": 144,
+                   "chi": 16, "clo": 16, "ones": 16, "vb": 3, "eb": 128, "ec": 128, "er": 128, "ez": 64},
+      "float32": {"yb": 4096, "jrow": 144, "jg": 128, "ir": 256, "iw": 256, "own0": 256, "own1": 128, "m16": 16, "cc": 64,
+                  "tmp3": 3, "of1": 16, "of2": 16, "st": 256},
+      "int32": {"ip": 1, "gi": 1, "ki": 1, "thi": 3, "gpi": 3}, "uint16": {}}
+for _t in range(3):
+    for _n, _k, _d in (("xc", XW, "bfloat16"), ("rh", HALO, "bfloat16"), ("last", HALO, "bfloat16"), ("dw", DWW, "bfloat16"),
+                       ("rm", RMW, "bfloat16"), ("sv", 144, "bfloat16"), ("pen", 128, "bfloat16"), ("q", 16, "float32"),
+                       ("lb", 128, "uint16"), ("lc", 128, "uint16"), ("lst", 20, "uint16"), ("off", 16, "uint16"),
+                       ("la", 64, "uint16"), ("ll", 64, "uint16"), ("slot", 128 if _t else 256, "uint16")):
+        _W[_d]["%s%d" % (_n, _t)] = _k
+SCRATCH = {n: ("sbuf", [128, k], d) for d, a in _W.items() for n, k in a.items()}
+SCRATCH["wb"] = ("sbuf", [128, 9, 16], "bfloat16")
+SCRATCH["wbd"] = ("sbuf", [128, 9, 128], "bfloat16")
+BANKS = ["b%d" % i for i in range(8)]
+for _b in BANKS:
+    SCRATCH[_b] = ("psum", [128, 512], "float32")
+SEMAPHORES = (["cv", "ca", "cp", "cg", "dv", "dt", "dg", "dwt", "sent"] + ["dx%d" % i for i in range(4)]
+              + ["dy%d" % i for i in range(8)] + ["al%d" % i for i in range(3)] + ["ar%d" % i for i in range(3)])
+PF, GF, KF, G15, K15, ND, SC, BI, BMIN, WL1, WL2, KLO = range(12)
+TH, GAP, BIAS, G16, VF, NG = 12, 15, 18, 21, 22, 25
+
+
+def tracker(g, T):
+    queues = {"v": g.vector, "a": g.scalar, "p": g.tensor, "g": g, "s": g.sync}
+    count, clock, order, recs, waited = {}, {}, {}, {}, {}
+    known = {e: {} for e in queues}
+    serial = [0]
+
+    def wait(eng, key, n):
+        if known[eng].get(key, 0) >= n:
+            return
+        queues[eng].wait_ge(T.sem[key], n)
+        waited[key] = max(waited.get(key, 0), n)
+        for k2, n2 in clock.get((key, n), {}).items():
+            known[eng][k2] = max(known[eng].get(k2, 0), n2)
+        known[eng][key] = n
+
+    def settle(eng, reads, writes):
+        need = {}
+        for kind, accs in (("r", reads), ("w", writes)):
+            for b, lo, hi in accs:
+                ps = b in BANKS
+                for rk, rlo, rhi, who, key, n in recs.get(b, ()):
+                    over = rlo < hi and lo < rhi
+                    if who == eng:
+                        if eng == "p" or not over or rk == kind == "r":
+                            continue
+                    elif not ps and (not over or rk == kind == "r"):
+                        continue
+                    need[key] = max(need.get(key, 0), n)
+        for key in sorted(need, key=lambda k: -order[(k, need[k])]):
+            wait(eng, key, need[key])
+
+    def note(who, key, n, reads, writes):
+        serial[0] += 1
+        order[(key, n)] = serial[0]
+        for kind, accs in (("r", reads), ("w", writes)):
+            for b, lo, hi in accs:
+                recs.setdefault(b, []).append((kind, lo, hi, who, key, n))
+
+    def emit(eng, fn, reads, writes, dma=None):
+        settle(eng, reads, writes)
+        key, step = (dma, 16) if dma else ("c" + eng, 1)
+        n = count.get(key, 0) + step
+        fn().then_inc(T.sem[key], step)
+        count[key] = n
+        clock[(key, n)] = dict(known[eng])
+        note("dma " + dma if dma else eng, key, n, reads, writes)
+
+    def remote(reads, key, n, fn):
+        settle("g", reads, [])
+        fn()
+        count[key] = count.get(key, 0) + n
+        note("net " + key, key, count[key], reads, [])
+
+    def landing(key, n, writes):
+        count[key] = n
+        note("net " + key, key, n, [], writes)
+
+    def finish():
+        for key in sorted(count):
+            if waited.get(key, 0) < count[key]:
+                wait("s", key, count[key])
+
+    return {"emit": emit, "remote": remote, "landing": landing, "finish": finish}
+
+
+def rank_program(g, core, T, topo):
+    rank = T.rank_of(core)
+    if rank is None:
+        return
+    tr = tracker(g, T)
+    emit = tr["emit"]
+    nranks = len(T.cores)
+
+    def S(name, lo, hi, step=1):
+        if step == 1:
+            return T[name][:, lo:hi], [(name, lo, hi)]
+        return T[name][:, lo:hi:step], [(name, lo, hi)]
+
+    def W(name, lo, hi, lname, l0, l1):
+        return T[name][:, lo:hi].indirect(T[lname][:, l0:l1]), [(name, lo, hi), (lname, l0, l1)]
+
+    def C(col):
+        return S("cc", col, col + 1)
+
+    def split(x):
+        return (x[0], x[1]) if isinstance(x, tuple) else (x, [])
+
+    def ts(out, in0, s1, s2, op0, op1=None):
+        (a1, r1), (a2, r2) = split(s1), split(s2)
+        if op1 is None:
+            emit("v", lambda: g.vector.tensor_scalar(out[0], in0[0], a1, None, op0), in0[1] + r1, out[1])
+        else:
+            emit("v", lambda: g.vector.tensor_scalar(out[0], in0[0], a1, a2, op0, op1), in0[1] + r1 + r2, out[1])
+
+    def tt(out, in0, in1, op):
+        emit("v", lambda: g.vector.tensor_tensor(out[0], in0[0], in1[0], op), in0[1] + in1[1], out[1])
+
+    def vcopy(out, in_):
+        emit("v", lambda: g.vector.tensor_copy(out[0], in_[0]), in_[1], out[1])
+
+    def vscatter(win, in_):
+        emit("v", lambda: g.vector.tensor_copy(win[0], in_[0]), in_[1] + win[1][1:], win[1][:1])
+
+    def vfill(out, c):
+        emit("v", lambda: g.vector.memset(out[0], c), [], out[1])
+
+    def scan(out, d0, d1, init, op0, op1):
+        ai, ri = split(init)
+        emit("v", lambda: g.vector.tensor_tensor_scan(out[0], d0[0], d1[0], ai, op0, op1), d0[1] + d1[1] + ri, out[1])
+
+    def act(out, in_, func, bias=0.0, scale=1.0):
+        (ab, rb), (asc, rs) = split(bias), split(scale)
+        emit("a", lambda: g.scalar.activation(out[0], in_[0], func, bias=ab, scale=asc), in_[1] + rb + rs, out[1])
+
+    def mms(items):
+        def go():
+            last = None
+            for o, l, r, a, b in items:
+                last = g.tensor.matmul(o[0], l[0], r[0], a, b)
+            return last
+        emit("p", go, sorted({a for i in items for a in i[1][1] + i[2][1]}), sorted({a for i in items for a in i[0][1]}))
+
+    def iota(name, lo, hi, pattern, base, cm):
+        if name == "ip":
+            emit("g", lambda: g.iota(T[name][:, lo:hi], pattern, base, cm), [], [(name, lo, hi)])
+        else:
+            emit("g", lambda: g.iota(T[name][:, lo:hi], pattern, base, cm, allow_small_or_imprecise_dtypes=True), [], [(name, lo, hi)])
+
+    def gfill(name, lo, hi, value):
+        iota(name, lo, hi, [[0, hi - lo]], value, 0)
+
+    def load(eng, sem, out, src):
+        q = g.sync if eng == "s" else g.scalar
+        emit(eng, lambda: q.dma_start(out[0], src), [], out[1], dma=sem)
+
+    def win(name, k):
+        return S(name, 15 - k, 143 - k)
+
+    def tap(t, j):
+        i = 3 * t + j
+        return T.wbd[:, i, :], [("wbd", i, i + 1)]
+
+    load("a", "dv", S("vb", 0, 3), T.v[:])
+    for c in range(4):
+        load("s", "dx%d" % c, S("big", 1024 * c, 1024 * c + 1024), T.x[:, 1024 * c:1024 * c + 1024])
+    load("a", "dt", S("thi", 0, 3), T.th[:])
+    load("a", "dg", S("gpi", 0, 3), T.gap[:])
+    load("a", "dwt", (T.wb[:, :, :], [("wb", 0, 9)]), T.w[:])
+
+    iota("ip", 0, 1, [[0, 1]], 0, 1)
+    iota("jrow", 0, 144, [[1, 144]], 0, 0)
+    iota("jg", 0, 128, [[1, 8], [0, 16]], 0, 0)
+    iota("ir", 0, 256, [[16, 256]], 0, 1)
+    iota("m16", 0, 16, [[16, 16]], 0, 0)
+    iota("mrow", 0, 256, [[1, 256]], 0, 0)
+    for t in range(3):
+        gfill("rm%d" % t, 0, 16, 0)
+    for t in range(3):
+        gfill("xc%d" % t, HALO + CAP, XW, 0)
+        zero = 0 if t == 0 else int(OFS)
+        if rank == 0:
+            gfill("xc%d" % t, 0, HALO, zero)
+        if rank == nranks - 1:
+            gfill("rh%d" % t, 0, HALO, zero)
+    gfill("dw1", 0, CAP, 0)
+    vfill(S("ones", 0, 16), 1.0)
+    ts(S("gi", 0, 1), S("ip", 0, 1), 4, None, OP.logical_shift_right)
+    ts(S("ki", 0, 1), S("ip", 0, 1), 15, None, OP.bitwise_and)
+    vcopy(C(PF), S("ip", 0, 1))
+    vcopy(C(GF), S("gi", 0, 1))
+    vcopy(C(KF), S("ki", 0, 1))
+    ts(C(G15), C(GF), 16.0, 15.0, OP.mult, OP.add)
+    ts(C(K15), C(KF), 15.0, None, OP.is_equal)
+    ts(S("e", 0, 144), S("jrow", 0, 144), C(G15), None, OP.is_equal)
+    vfill(S("dw0", 0, CAP), 0.0)
+    ts(S("sv0", 0, 144), S("e", 0, 144), S("vb", 0, 1), None, OP.mult)
+    for col, sc, bi in ((ND, 1.0, -1.0), (SC, 2.0, -1.0), (BI, -1.0, 1.0), (BMIN, 255.0, 1.0), (WL1, 15.0, 1.0), (WL2, 17.0, -1.0)):
+        act(C(col), C(K15), AF.Identity, bias=bi, scale=sc)
+    act(C(G16), C(GF), AF.Copy, scale=-16.0)
+    act(C(KLO), C(KF), AF.Copy, scale=-1.0 / 8192)
+    act(S("dc", 0, CAP), S("dw0", 0, CAP), AF.Identity, bias=C(ND))
+    ts(S("bd", 0, 128), S("jg", 0, 128), C(GF), None, OP.is_equal)
+    ts(S("ltf", 0, 128), S("jrow", 0, 128), C(PF), None, OP.is_ge)
+    ts(S("idn", 0, 128), S("jrow", 0, 128), C(PF), None, OP.is_equal)
+    tt(S("ltf", 0, 128), S("ltf", 0, 128), S("bd", 0, 128), OP.mult)
+    ts(S("s15", 0, 128), S("idn", 0, 128), C(K15), None, OP.mult)
+    tt(S("lt", 0, 128), S("ltf", 0, 128), S("e", 0, 128), OP.subtract)
+    ts(S("idk", 0, 128), S("idn", 0, 128), 8192.0, None, OP.mult)
+    vcopy(S("cc", TH, TH + 3), S("thi", 0, 3))
+    vcopy(S("cc", GAP, GAP + 3), S("gpi", 0, 3))
+    vcopy(S("cc", VF, VF + 3), S("vb", 0, 3))
+    ts(S("cc", NG, NG + 3), S("cc", GAP, GAP + 3), -1.0, None, OP.mult)
+    ts(S("iw", 0, 256), S("ir", 0, 256), C(G16), None, OP.add)
+    ts(S("chi", 0, 16), S("m16", 0, 16), 2048.0, -1.0 / 8192, OP.add, OP.mult)
+    ts(S("clo", 0, 16), S("m16", 0, 16), 0.0, C(KLO), OP.mult, OP.add)
+    act(S("el1", 0, 144), S("e", 0, 144), AF.Copy, scale=C(WL1))
+    act(S("el2", 0, 144), S("e", 0, 144), AF.Copy, scale=C(WL2))
+    for t in (1, 2):
+        act(S("sv%d" % t, 0, 144), S("e", 0, 144), AF.Copy, scale=C(VF + t))
+    for t in range(3):
+        iw4, q = S("iw", 0, 4), "q%d" % t
+        act(S(q, 4, 8), iw4, AF.Identity, bias=C(NG + t))
+        act(S(q, 8, 12), iw4, AF.Identity, bias=-64.0)
+        act(S(q, 12, 16), iw4, AF.Identity, bias=C(GAP + t))
+    base = [4096 - 1 - 8192, 2048 - 1 - 8192]
+    for i, n in ((0, 256), (1, 128)):
+        act(S("own%d" % i, 0, n), S("iw", 0, n), AF.Identity, bias=float(-base[i]))
+    for gg in range(8):
+        emit("v", lambda: g.vector.tensor_scalar(T.wbd[:, :, 16 * gg:16 * gg + 16], T.wb[:, :, :], T.bd[:, 16 * gg:16 * gg + 1], None, OP.mult),
+             [("wb", 0, 9), ("bd", 16 * gg, 16 * gg + 1)], [("wbd", 0, 9)] if gg == 7 else [])
+
+    def shift_lists(t):
+        l, iw4 = "lst%d" % t, S("iw", 0, 4)
+        ts(S(l, 0, 4), iw4, C(GAP + t), 64.0, OP.subtract, OP.add)
+        ts(S(l, 16, 20), iw4, C(GAP + t), 64.0, OP.add, OP.add)
+        ts(S("lb%d" % t, 4, 128), S("iw", 4, 128), C(GAP + t), None, OP.subtract)
+        ts(S("lc%d" % t, 4, 128), S("iw", 4, 128), C(GAP + t), None, OP.add)
+
+    def slots_a(t):
+        n = 128 if t else 256
+        tt(S("st", 0, n), S("own%d" % (t > 0), 0, n), S("b3", 16, 16 + n), OP.max)
+
+    def slots_b(t):
+        n = 128 if t else 256
+        ts(S("slot%d" % t, 0, n), S("st", 0, n), float(base[t > 0]), None, OP.add)
+
+    zoff = [Z1, Z2, Z3]
+
+    def send(t):
+        x, la = "xc%d" % t, "last%d" % t
+        out = []
+        if rank > 0:
+            out.append((rank - 1, S(x, HALO, 2 * HALO), T["rh%d" % t][:, 0:HALO], "ar%d" % t))
+        if rank < nranks - 1:
+            out.append((rank + 1, S(la, 0, HALO), T[x][:, 0:HALO], "al%d" % t))
+        reads = [a for o in out for a in o[1][1]]
+        if len(out) == 1:
+            dst = T.cores[out[0][0]]
+            a = topo.addr(dst)
+            tr["remote"](reads, "sent", len(topo.engines(core, dst)), lambda: g.remote_dma(
+                out_ap=out[0][2], in_ap=out[0][1][0], remote_sem=T.sem[out[0][3]], local_sem=T.sem.sent,
+                pid=a[1], routing_id=a[0], dma_engine_mask=topo.mask(core, dst)))
+            return
+        trs, used = [], 0
+        for i, o in enumerate(out):
+            dst = T.cores[o[0]]
+            a = topo.addr(dst)
+            en = topo.engines(core, dst)
+            half = len(en) // 2
+            mine = en[:half] if i == 0 else en[half:]
+            used += len(mine)
+            trs.append(RemoteDMATransfer(dst_ids=[DstId(rid=a[0], pnc=a[1])], dma_engine_mask=sum(1 << k for k in mine),
+                                         remote_sem=T.sem[o[3]], src=o[1][0], dst=o[2]))
+        tr["remote"](reads, "sent", used, lambda: g.remote_dma_fused(trs, local_sem=T.sem.sent))
+
+    for t in range(3):
+        for peer, key, acc in ((rank - 1, "al%d" % t, ("xc%d" % t, 0, HALO)), (rank + 1, "ar%d" % t, ("rh%d" % t, 0, HALO))):
+            if 0 <= peer < nranks:
+                en = len(topo.engines(T.cores[peer], core))
+                tr["landing"](key, en if peer in (0, nranks - 1) else en // 2, [acc])
+
+    for t in range(3):
+        nb = 256 if t == 0 else 128
+        nw = nb // 16
+        rm, dw, xc, lst, last, sv = ["%s%d" % (n, t) for n in ("rm", "dw", "xc", "lst", "last", "sv")]
+        src0, srcn = (0, 4096) if t == 0 else (zoff[t - 1], CAP)
+        M0, R0 = 16, 16 + nb
+        if t == 0:
+            for c in range(4):
+                ob = S("b0", 64 * c, 64 * c + 64) if c < 3 else S("b3", 0, 64)
+                mms([(ob, win(sv, k), S("big", 1024 * c + k, 1024 * c + 1024, 16), k == 0, k == 15) for k in range(16)])
+                if c == 2:
+                    ts(S(rm, M0, M0 + 192), S("b0", 0, 192), C(TH), None, OP.is_ge)
+            ts(S(rm, M0 + 192, M0 + 256), S("b3", 0, 64), C(TH), None, OP.is_ge)
+        else:
+            mms([(S("b0", 0, nb), S("idn", 0, 128), S("pen%d" % t, 0, 128), True, False)]
+                + [(S("b0", 0, nb), win(sv, k), S("big", src0 + k, src0 + CAP, 16), False, k == 15) for k in range(16)])
+            if t == 1:
+                ts(S("tmp3", 1, 3), S("b2", 1, 3), OFS, None, OP.mult)
+                tt(S("cc", TH + 1, TH + 3), S("cc", TH + 1, TH + 3), S("tmp3", 1, 3), OP.add)
+                for i in (1, 2):
+                    ts(C(BIAS + i), S("b2", 4 * i, 4 * i + 1), -24.0, OFS, OP.mult, OP.add)
+            shift_lists(t)
+            ts(S(rm, M0, M0 + nb), S("b0", 0, nb), C(TH + t), None, OP.is_ge)
+        mms([(S("b1", 0, nb), S("lt", 0, 128), S(rm, M0, M0 + nb), True, False),
+             (S("b1", 0, nb), S("s15", 0, 128), S("mrow", 0, nb), False, True)])
+        scan(S(rm, R0, R0 + nb + 1), S(rm, M0 - 1, M0 + nb), S(rm, M0 - 1, M0 + nb), 0.0, OP.add, OP.max)
+        act(S("dsb", 0, nb), S("b1", 0, nb), AF.Copy)
+        if t == 0:
+            shift_lists(0)
+        else:
+            slots_a(t - 1)
+        b2 = S("b2", 0, 2 * nw)
+        rhs = [(win("e", k), S(rm, M0 + k, M0 + 2 * nb, 16)) for k in range(16)]
+        mms([(b2, rhs[0][0], rhs[0][1], True, False),
+             (S("b2", 0, nw), S("idn", 0, 128), S("chi", 0, nw), False, False), (S("b2", 0, nw), S("idn", 0, 128), S("clo", 0, nw), False, False)]
+            + [(b2, rhs[k][0], rhs[k][1], False, k == 15) for k in range(1, 16)])
+        mms([(S("b3", 0, 1), S("bd", 0, 128), S(rm, R0 + nb, R0 + nb + 1), True, True)])
+        ts(S("of1", 0, nw), S("b2", 0, nw), -8192.0, None, OP.mult)
+        tt(S("of2", 0, nw), S("of1", 0, nw), S("b2", nw, 2 * nw), OP.max)
+        vcopy(S("off%d" % t, 0, nw), S("of2", 0, nw))
+        vscatter(W(dw, 0, DWW, "off%d" % t, 0, nw), S("dsb", 0, nb))
+        cum = S("b3", 16, 16 + nb)
+        mms([(cum, S("bd", 0, 128), S(rm, R0, R0 + nb), True, False), (cum, S("ltf", 0, 128), S(rm, M0, M0 + nb), False, False),
+             (cum, S("idk", 0, 128), S(rm, M0, M0 + nb), False, True)])
+        u0 = 0.0
+        for lo, hi in ((0, 512), (512, 1024), (1024, 2048)):
+            scan(S("u", lo, hi), S("dc", lo, hi), S(dw, lo, hi), u0, OP.add, OP.max)
+            if lo < 1024:
+                act(S("cb", lo, hi), S("u", lo, hi), AF.Relu, bias=C(BI), scale=C(SC))
+            u0 = S("u", hi - 1, hi)
+        ts(S("cb", 1024, 2048), S("u", 1024, 2048), C(BMIN), None, OP.min)
+        ts(S(lst, 4, 16), S("q%d" % t, 4, 16), S("b3", 0, 1), None, OP.add)
+        if t < 2:
+            ts(S("pen%d" % (t + 1), 0, 128), S("iw", 0, 128), S("b3", 0, 1), -32768.0, OP.is_ge, OP.mult)
+        mms([(S("b1", 0, 64), win("el1", k), S("cb", k, 1024, 16), k == 0, k == 15) for k in range(16)])
+        mms([(S("b0", 0, 64), win("el2", k), S("cb", 1024 + k, 2048, 16), k == 0, k == 15) for k in range(16)])
+        vcopy(S("la%d" % t, 0, 64), S("b1", 0, 64))
+        act(S(xc, 64, 1088), W("big", src0, src0 + srcn, "la%d" % t, 0, 64), AF.Copy)
+        if t:
+            slots_b(t - 1)
+        ts(S("ll%d" % t, 0, 64), S("b0", 0, 64), 15.0, None, OP.add)
+        vcopy(S(xc, 1088, 2112), W("big", src0, src0 + srcn, "ll%d" % t, 0, 64))
+        vcopy(S(last, 0, HALO), W(xc, HALO, XW, lst, 8, 12))
+        send(t)
+        z = zoff[t]
+        bias = OFS if t == 0 else C(BIAS + t)
+        ch4 = [(64, 512), (512, 1024), (1024, 1536), (1536, 2048)]
+
+        def left(c):
+            lo, hi = ch4[c]
+            vcopy(S("gb", lo, hi), W(xc, HALO, HALO + CAP, "lb%d" % t, lo // 16, hi // 16))
+
+        def right(c):
+            lo, hi = ch4[c]
+            act(S("gc", lo, hi), W(xc, HALO, XW, "lc%d" % t, lo // 16, hi // 16), AF.Copy)
+
+        def mix(c):
+            lo, hi = ch4[c]
+            o = S("b%d" % (4 + c), 0, hi - lo)
+            mms([(o, tap(t, 0), S(xc, HALO + lo, HALO + hi), True, False)])
+            mms([(o, tap(t, 1), S("gb", lo, hi), False, False), (o, tap(t, 2), S("gc", lo, hi), False, True)])
+
+        def near(c, eng, lo, hi):
+            i = S("b%d" % (4 + c), lo - ch4[c][0], hi - ch4[c][0])
+            if eng == "a":
+                act(S("zr", lo, hi), i, AF.Identity, bias=bias, scale=0.125)
+            else:
+                ts(S("zr", lo, hi), i, 0.125, bias, OP.mult, OP.add)
+
+        def clamp(lo, hi):
+            ts(S("big", z + lo, z + hi), S("zr", lo, hi), OFS - 15.0, OFS + 15.0, OP.max, OP.min)
+
+        right(0); left(0); mix(0)
+        right(1); left(1); mix(1)
+        near(0, "a", 64, 512); left(2); right(2); mix(2)
+        near(1, "a", 512, 1024); clamp(64, 512); left(3); right(3); mix(3)
+        clamp(512, 1024)
+        near(2, "v", 1024, 1536)
+        clamp(1024, 1536)
+        near(3, "a", 1536, 2048)
+        if t == 0:
+            mms([(S("b2", 0, 3), S("bd", 0, 128), S("vb", 0, 3), True, True)]
+                + [(S("b2", 4 * i, 4 * i + 1), tap(i, j), S("ones", 0, 1), j == 0, j == 2) for i in (1, 2) for j in range(3)])
+            gfill("dw2", 0, CAP, 0)
+        if t == 2:
+            slots_a(2)
+            slots_b(2)
+        clamp(1536, 2048)
+        vscatter(W(xc, 2 * HALO, XW, lst, 8, 12), S("rh%d" % t, 0, HALO))
+        act(S("ec", 0, 128), W(xc, 0, XW, lst, 12, 20), AF.Copy)
+        vcopy(S("eb", 0, 128), W(xc, 0, XW, lst, 0, 8))
+        mms([(S("b1", 0, 64), tap(t, 0), S(xc, HALO, 2 * HALO), True, False),
+             (S("b1", 0, 64), tap(t, 1), S("eb", 0, 64), False, False),
+             (S("b1", 0, 64), tap(t, 2), S("ec", 64, 128), False, True),
+             (S("b1", 64, 128), tap(t, 0), S(last, 0, HALO), True, False),
+             (S("b1", 64, 128), tap(t, 1), S("eb", 64, 128), False, False),
+             (S("b1", 64, 128), tap(t, 2), S("ec", 0, 64), False, True)])
+        ts(S("er", 0, 128), S("b1", 0, 128), 0.125, bias, OP.mult, OP.add)
+        ts(S("ez", 0, 64), S("er", 64, 128), OFS - 15.0, OFS + 15.0, OP.max, OP.min)
+        ts(S("big", z, z + 64), S("er", 0, 64), OFS - 15.0, OFS + 15.0, OP.max, OP.min)
+        vscatter(W("big", z, z + CAP, lst, 8, 12), S("ez", 0, 64))
+
+    act(S("big", V2, V2 + 1024), W("big", Z2, Z2 + 4096, "slot2", 0, 64), AF.Copy)
+    vcopy(S("big", V2 + 1024, V2 + 2048), W("big", Z2, Z2 + 4096, "slot2", 64, 128))
+    act(S("big", V1, V1 + 1024), W("big", Z1, Z1 + 4096, "slot1", 0, 64), AF.Identity, bias=-OFS)
+    ts(S("big", V1 + 1024, V1 + 2048), W("big", Z1, Z1 + 4096, "slot1", 64, 128), -OFS, None, OP.add)
+    for c in range(8):
+        o, i = S("yb", 512 * c, 512 * c + 512), W("big", 0, 6144, "slot0", 32 * c, 32 * c + 32)
+        if c % 2:
+            act(o, i, AF.Copy)
+        else:
+            vcopy(o, i)
+        emit("s", lambda: g.sync.dma_start(T.y[:, 512 * c:512 * c + 512], T.yb[:, 512 * c:512 * c + 512]),
+             [("yb", 512 * c, 512 * c + 512)], [], dma="dy%d" % c)
+    tr["finish"]()

@@ -10,15 +10,15 @@ DWW, RMW = CAP + 256, 544
 
 _W = {"bfloat16": {"big": BIGW, "gb": CAP, "gc": CAP, "zr": CAP, "u": CAP, "cb": CAP, "dc": CAP, "dsb": 256, "mrow": 256,
                    "e": 144, "bd": 128, "idn": 128, "idk": 128, "ltf": 128, "lt": 128, "s15": 128, "el1": 144, "el2": 144,
-                   "chi": 16, "clo": 16, "ones": 16, "vb": 3, "eb": 128, "ec": 128, "er": 128, "ez": 64},
-      "float32": {"yb": 4096, "jrow": 144, "jg": 128, "ir": 256, "iw": 256, "own0": 256, "own1": 128, "m16": 16, "cc": 64,
-                  "tmp3": 3, "of1": 16, "of2": 16, "st": 256},
+                   "chi": 16, "clo": 16, "ones": 16, "vb": 3, "eb": 128, "ec": 128, "er": 128, "ez": 64, "cf": 128},
+      "float32": {"yb": 4096, "jrow": 144, "jg": 128, "ir": 256, "iw": 256, "own0": 256, "own1": 128, "m16": 16, "g8": 8, "gm": 8,
+                  "cc": 64, "tmp3": 3, "of1": 16, "of2": 16, "st": 256, "pm": 8, "qr": 12},
       "int32": {"ip": 1, "gi": 1, "ki": 1, "thi": 3, "gpi": 3}, "uint16": {}}
 for _t in range(3):
-    for _n, _k, _d in (("xc", XW, "bfloat16"), ("rh", HALO, "bfloat16"), ("last", HALO, "bfloat16"), ("dw", DWW, "bfloat16"),
-                       ("rm", RMW, "bfloat16"), ("sv", 144, "bfloat16"), ("pen", 128, "bfloat16"), ("q", 16, "float32"),
-                       ("lb", 128, "uint16"), ("lc", 128, "uint16"), ("lst", 20, "uint16"), ("off", 16, "uint16"),
-                       ("la", 64, "uint16"), ("ll", 64, "uint16"), ("slot", 128 if _t else 256, "uint16")):
+    for _n, _k, _d in (("xc", XW + HALO, "bfloat16"), ("fl", 2 * HALO, "bfloat16"), ("dw", DWW, "bfloat16"), ("rm", RMW, "bfloat16"),
+                       ("sv", 144, "bfloat16"), ("pen", 128, "bfloat16"), ("q", 12, "float32"), ("pc", 8, "float32"),
+                       ("lb", 128, "uint16"), ("lc", 128, "uint16"), ("lst", 12, "uint16"), ("lec", 8, "uint16"), ("fll", 8, "uint16"),
+                       ("off", 16, "uint16"), ("la", 64, "uint16"), ("ll", 64, "uint16"), ("slot", 128 if _t else 256, "uint16")):
         _W[_d]["%s%d" % (_n, _t)] = _k
 SCRATCH = {n: ("sbuf", [128, k], d) for d, a in _W.items() for n, k in a.items()}
 SCRATCH["wb"] = ("sbuf", [128, 9, 16], "bfloat16")
@@ -29,7 +29,7 @@ for _b in BANKS:
 SEMAPHORES = (["cv", "ca", "cp", "cg", "dv", "dt", "dg", "dwt", "sent"] + ["dx%d" % i for i in range(4)]
               + ["dy%d" % i for i in range(8)] + ["al%d" % i for i in range(3)] + ["ar%d" % i for i in range(3)])
 PF, GF, KF, G15, K15, ND, SC, BI, BMIN, WL1, WL2, KLO = range(12)
-TH, GAP, BIAS, G16, VF, NG = 12, 15, 18, 21, 22, 25
+TH, GAP, BIAS, G16, VF, NG, KC, KR = 12, 15, 18, 21, 22, 25, 28, 29
 
 
 def tracker(g, T):
@@ -187,6 +187,7 @@ def rank_program(g, core, T, topo):
     iota("ir", 0, 256, [[16, 256]], 0, 1)
     iota("m16", 0, 16, [[16, 16]], 0, 0)
     iota("mrow", 0, 256, [[1, 256]], 0, 0)
+    iota("g8", 0, 8, [[1, 8]], 0, 0)
     for t in range(3):
         gfill("rm%d" % t, 0, 16, 0)
     for t in range(3):
@@ -195,7 +196,7 @@ def rank_program(g, core, T, topo):
         if rank == 0:
             gfill("xc%d" % t, 0, HALO, zero)
         if rank == nranks - 1:
-            gfill("rh%d" % t, 0, HALO, zero)
+            gfill("xc%d" % t, XW, XW + HALO, zero)
     gfill("dw1", 0, CAP, 0)
     vfill(S("ones", 0, 16), 1.0)
     ts(S("gi", 0, 1), S("ip", 0, 1), 4, None, OP.logical_shift_right)
@@ -220,6 +221,7 @@ def rank_program(g, core, T, topo):
     ts(S("s15", 0, 128), S("idn", 0, 128), C(K15), None, OP.mult)
     tt(S("lt", 0, 128), S("ltf", 0, 128), S("e", 0, 128), OP.subtract)
     ts(S("idk", 0, 128), S("idn", 0, 128), 8192.0, None, OP.mult)
+    ts(S("gm", 0, 8), S("g8", 0, 8), C(GF), None, OP.is_equal)
     vcopy(S("cc", TH, TH + 3), S("thi", 0, 3))
     vcopy(S("cc", GAP, GAP + 3), S("gpi", 0, 3))
     vcopy(S("cc", VF, VF + 3), S("vb", 0, 3))
@@ -235,18 +237,17 @@ def rank_program(g, core, T, topo):
         iw4, q = S("iw", 0, 4), "q%d" % t
         act(S(q, 4, 8), iw4, AF.Identity, bias=C(NG + t))
         act(S(q, 8, 12), iw4, AF.Identity, bias=-64.0)
-        act(S(q, 12, 16), iw4, AF.Identity, bias=C(GAP + t))
+        act(S("pc%d" % t, 0, 4), iw4, AF.Identity, bias=C(GAP + t))
+        act(S("qr", 4 * t, 4 * t + 4), S(q, 8, 12), AF.Identity, bias=C(GAP + t))
     base = [4096 - 1 - 8192, 2048 - 1 - 8192]
     for i, n in ((0, 256), (1, 128)):
         act(S("own%d" % i, 0, n), S("iw", 0, n), AF.Identity, bias=float(-base[i]))
-    for gg in range(8):
-        emit("v", lambda: g.vector.tensor_scalar(T.wbd[:, :, 16 * gg:16 * gg + 16], T.wb[:, :, :], T.bd[:, 16 * gg:16 * gg + 1], None, OP.mult),
-             [("wb", 0, 9), ("bd", 16 * gg, 16 * gg + 1)], [("wbd", 0, 9)] if gg == 7 else [])
+    for i in range(8):
+        emit("a", lambda: g.scalar.activation(T.wbd[:, :, 16 * i:16 * i + 16], T.wb[:, :, :], AF.Copy, scale=T.gm[:, i:i + 1]),
+             [("wb", 0, 9), ("gm", i, i + 1)], [("wbd", 0, 9)] if i == 7 else [])
 
     def shift_lists(t):
-        l, iw4 = "lst%d" % t, S("iw", 0, 4)
-        ts(S(l, 0, 4), iw4, C(GAP + t), 64.0, OP.subtract, OP.add)
-        ts(S(l, 16, 20), iw4, C(GAP + t), 64.0, OP.add, OP.add)
+        ts(S("lst%d" % t, 0, 4), S("iw", 0, 4), C(GAP + t), 64.0, OP.subtract, OP.add)
         ts(S("lb%d" % t, 4, 128), S("iw", 4, 128), C(GAP + t), None, OP.subtract)
         ts(S("lc%d" % t, 4, 128), S("iw", 4, 128), C(GAP + t), None, OP.add)
 
@@ -261,12 +262,12 @@ def rank_program(g, core, T, topo):
     zoff = [Z1, Z2, Z3]
 
     def send(t):
-        x, la = "xc%d" % t, "last%d" % t
+        fl, x = "fl%d" % t, "xc%d" % t
         out = []
         if rank > 0:
-            out.append((rank - 1, S(x, HALO, 2 * HALO), T["rh%d" % t][:, 0:HALO], "ar%d" % t))
+            out.append((rank - 1, S(fl, 0, HALO), T[x][:, XW:XW + HALO], "ar%d" % t))
         if rank < nranks - 1:
-            out.append((rank + 1, S(la, 0, HALO), T[x][:, 0:HALO], "al%d" % t))
+            out.append((rank + 1, S(fl, HALO, 2 * HALO), T[x][:, 0:HALO], "al%d" % t))
         reads = [a for o in out for a in o[1][1]]
         if len(out) == 1:
             dst = T.cores[out[0][0]]
@@ -288,15 +289,15 @@ def rank_program(g, core, T, topo):
         tr["remote"](reads, "sent", used, lambda: g.remote_dma_fused(trs, local_sem=T.sem.sent))
 
     for t in range(3):
-        for peer, key, acc in ((rank - 1, "al%d" % t, ("xc%d" % t, 0, HALO)), (rank + 1, "ar%d" % t, ("rh%d" % t, 0, HALO))):
+        for peer, key, lo in ((rank - 1, "al%d" % t, 0), (rank + 1, "ar%d" % t, XW)):
             if 0 <= peer < nranks:
                 en = len(topo.engines(T.cores[peer], core))
-                tr["landing"](key, en if peer in (0, nranks - 1) else en // 2, [acc])
+                tr["landing"](key, en if peer in (0, nranks - 1) else en // 2, [("xc%d" % t, lo, lo + HALO)])
 
     for t in range(3):
         nb = 256 if t == 0 else 128
         nw = nb // 16
-        rm, dw, xc, lst, last, sv = ["%s%d" % (n, t) for n in ("rm", "dw", "xc", "lst", "last", "sv")]
+        rm, dw, xc, lst, fl, sv = ["%s%d" % (n, t) for n in ("rm", "dw", "xc", "lst", "fl", "sv")]
         src0, srcn = (0, 4096) if t == 0 else (zoff[t - 1], CAP)
         M0, R0 = 16, 16 + nb
         if t == 0:
@@ -310,10 +311,10 @@ def rank_program(g, core, T, topo):
             mms([(S("b0", 0, nb), S("idn", 0, 128), S("pen%d" % t, 0, 128), True, False)]
                 + [(S("b0", 0, nb), win(sv, k), S("big", src0 + k, src0 + CAP, 16), False, k == 15) for k in range(16)])
             if t == 1:
-                ts(S("tmp3", 1, 3), S("b2", 1, 3), OFS, None, OP.mult)
+                ts(S("tmp3", 1, 3), S("b2", 9, 11), OFS, None, OP.mult)
                 tt(S("cc", TH + 1, TH + 3), S("cc", TH + 1, TH + 3), S("tmp3", 1, 3), OP.add)
                 for i in (1, 2):
-                    ts(C(BIAS + i), S("b2", 4 * i, 4 * i + 1), -24.0, OFS, OP.mult, OP.add)
+                    ts(C(BIAS + i), S("b2", 8 + 4 * i, 9 + 4 * i), -24.0, OFS, OP.mult, OP.add)
             shift_lists(t)
             ts(S(rm, M0, M0 + nb), S("b0", 0, nb), C(TH + t), None, OP.is_ge)
         mms([(S("b1", 0, nb), S("lt", 0, 128), S(rm, M0, M0 + nb), True, False),
@@ -334,6 +335,9 @@ def rank_program(g, core, T, topo):
         tt(S("of2", 0, nw), S("of1", 0, nw), S("b2", nw, 2 * nw), OP.max)
         vcopy(S("off%d" % t, 0, nw), S("of2", 0, nw))
         vscatter(W(dw, 0, DWW, "off%d" % t, 0, nw), S("dsb", 0, nb))
+        act(C(KR), S("b3", 0, 1), AF.Copy)
+        act(C(KC), C(KR), AF.Identity, bias=float(XW - HALO), scale=-1.0)
+        act(S("pc%d" % t, 4, 8), S("qr", 4 * t, 4 * t + 4), AF.Identity, bias=C(KR))
         cum = S("b3", 16, 16 + nb)
         mms([(cum, S("bd", 0, 128), S(rm, R0, R0 + nb), True, False), (cum, S("ltf", 0, 128), S(rm, M0, M0 + nb), False, False),
              (cum, S("idk", 0, 128), S(rm, M0, M0 + nb), False, True)])
@@ -342,11 +346,17 @@ def rank_program(g, core, T, topo):
             scan(S("u", lo, hi), S("dc", lo, hi), S(dw, lo, hi), u0, OP.add, OP.max)
             if lo < 1024:
                 act(S("cb", lo, hi), S("u", lo, hi), AF.Relu, bias=C(BI), scale=C(SC))
+            if lo == 0:
+                ts(S(lst, 4, 12), S("q%d" % t, 4, 12), C(KR), None, OP.add)
+            if lo == 512:
+                ts(S("cf", 0, 64), S("u", 0, 64), C(BMIN), None, OP.min)
             u0 = S("u", hi - 1, hi)
+        ts(S("cf", 64, 128), W("u", 0, CAP, lst, 8, 12), C(BMIN), None, OP.min)
+        mms([(S("b2", 0, 8), win("el2", k), S("cf", k, 128, 16), k == 0, k == 15) for k in range(16)])
         ts(S("cb", 1024, 2048), S("u", 1024, 2048), C(BMIN), None, OP.min)
-        ts(S(lst, 4, 16), S("q%d" % t, 4, 16), S("b3", 0, 1), None, OP.add)
-        if t < 2:
-            ts(S("pen%d" % (t + 1), 0, 128), S("iw", 0, 128), S("b3", 0, 1), -32768.0, OP.is_ge, OP.mult)
+        ts(S("fll%d" % t, 0, 8), S("b2", 0, 8), 15.0, None, OP.add)
+        vcopy(S(fl, 0, 128), W("big", src0, src0 + srcn, "fll%d" % t, 0, 8))
+        send(t)
         mms([(S("b1", 0, 64), win("el1", k), S("cb", k, 1024, 16), k == 0, k == 15) for k in range(16)])
         mms([(S("b0", 0, 64), win("el2", k), S("cb", 1024 + k, 2048, 16), k == 0, k == 15) for k in range(16)])
         vcopy(S("la%d" % t, 0, 64), S("b1", 0, 64))
@@ -355,76 +365,86 @@ def rank_program(g, core, T, topo):
             slots_b(t - 1)
         ts(S("ll%d" % t, 0, 64), S("b0", 0, 64), 15.0, None, OP.add)
         vcopy(S(xc, 1088, 2112), W("big", src0, src0 + srcn, "ll%d" % t, 0, 64))
-        vcopy(S(last, 0, HALO), W(xc, HALO, XW, lst, 8, 12))
-        send(t)
         z = zoff[t]
         bias = OFS if t == 0 else C(BIAS + t)
-        ch4 = [(64, 512), (512, 1024), (1024, 1536), (1536, 2048)]
+        ch = [(64, 512), (512, 1024), (1024, 1536), (1536, 1856), (1856, 2048)]
 
         def left(c):
-            lo, hi = ch4[c]
+            lo, hi = ch[c]
             vcopy(S("gb", lo, hi), W(xc, HALO, HALO + CAP, "lb%d" % t, lo // 16, hi // 16))
 
-        def right(c):
-            lo, hi = ch4[c]
-            act(S("gc", lo, hi), W(xc, HALO, XW, "lc%d" % t, lo // 16, hi // 16), AF.Copy)
+        def right(c, eng="a"):
+            lo, hi = ch[c]
+            o, i = S("gc", lo, hi), W(xc, HALO, XW, "lc%d" % t, lo // 16, hi // 16)
+            act(o, i, AF.Copy) if eng == "a" else vcopy(o, i)
+
+        def bank(c):
+            return S("b%d" % (4 + c % 4), 0, ch[c][1] - ch[c][0])
 
         def mix(c):
-            lo, hi = ch4[c]
-            o = S("b%d" % (4 + c), 0, hi - lo)
-            mms([(o, tap(t, 0), S(xc, HALO + lo, HALO + hi), True, False)])
-            mms([(o, tap(t, 1), S("gb", lo, hi), False, False), (o, tap(t, 2), S("gc", lo, hi), False, True)])
+            lo, hi = ch[c]
+            mms([(bank(c), tap(t, 0), S(xc, HALO + lo, HALO + hi), True, False)])
+            mms([(bank(c), tap(t, 1), S("gb", lo, hi), False, False)])
+            mms([(bank(c), tap(t, 2), S("gc", lo, hi), False, True)])
 
-        def near(c, eng, lo, hi):
-            i = S("b%d" % (4 + c), lo - ch4[c][0], hi - ch4[c][0])
+        def near(c, eng="a"):
+            lo, hi = ch[c]
             if eng == "a":
-                act(S("zr", lo, hi), i, AF.Identity, bias=bias, scale=0.125)
+                act(S("zr", lo, hi), bank(c), AF.Identity, bias=bias, scale=0.125)
             else:
-                ts(S("zr", lo, hi), i, 0.125, bias, OP.mult, OP.add)
+                ts(S("zr", lo, hi), bank(c), 0.125, bias, OP.mult, OP.add)
 
-        def clamp(lo, hi):
+        def clamp(c):
+            lo, hi = ch[c]
             ts(S("big", z + lo, z + hi), S("zr", lo, hi), OFS - 15.0, OFS + 15.0, OP.max, OP.min)
 
         right(0); left(0); mix(0)
         right(1); left(1); mix(1)
-        near(0, "a", 64, 512); left(2); right(2); mix(2)
-        near(1, "a", 512, 1024); clamp(64, 512); left(3); right(3); mix(3)
-        clamp(512, 1024)
-        near(2, "v", 1024, 1536)
-        clamp(1024, 1536)
-        near(3, "a", 1536, 2048)
-        if t == 0:
-            mms([(S("b2", 0, 3), S("bd", 0, 128), S("vb", 0, 3), True, True)]
-                + [(S("b2", 4 * i, 4 * i + 1), tap(i, j), S("ones", 0, 1), j == 0, j == 2) for i in (1, 2) for j in range(3)])
-            gfill("dw2", 0, CAP, 0)
+        near(0); left(2); right(2); mix(2)
+        near(1); clamp(0); left(3); right(3); mix(3)
+        left(4); right(4, "v"); mix(4)
+        near(2); near(3)
+        ts(S("pm", 0, 8), S("pc%d" % t, 0, 8), C(KR), C(KC), OP.is_ge, OP.mult)
+        clamp(1)
+        tt(S("pm", 0, 8), S("pm", 0, 8), S("pc%d" % t, 0, 8), OP.add)
+        if t < 2:
+            ts(S("pen%d" % (t + 1), 0, 128), S("iw", 0, 128), C(KR), -32768.0, OP.is_ge, OP.mult)
+        ts(S("lec%d" % t, 0, 8), S("pm", 0, 8), 64.0, None, OP.add)
         if t == 2:
             slots_a(2)
             slots_b(2)
-        clamp(1536, 2048)
-        vscatter(W(xc, 2 * HALO, XW, lst, 8, 12), S("rh%d" % t, 0, HALO))
-        act(S("ec", 0, 128), W(xc, 0, XW, lst, 12, 20), AF.Copy)
-        vcopy(S("eb", 0, 128), W(xc, 0, XW, lst, 0, 8))
-        mms([(S("b1", 0, 64), tap(t, 0), S(xc, HALO, 2 * HALO), True, False),
-             (S("b1", 0, 64), tap(t, 1), S("eb", 0, 64), False, False),
-             (S("b1", 0, 64), tap(t, 2), S("ec", 64, 128), False, True),
-             (S("b1", 64, 128), tap(t, 0), S(last, 0, HALO), True, False),
-             (S("b1", 64, 128), tap(t, 1), S("eb", 64, 128), False, False),
-             (S("b1", 64, 128), tap(t, 2), S("ec", 0, 64), False, True)])
+        near(4, "v")
+        clamp(2)
+        if t == 0:
+            mms([(S("b2", 8, 11), S("bd", 0, 128), S("vb", 0, 3), True, True)]
+                + [(S("b2", 8 + 4 * i, 9 + 4 * i), tap(i, j), S("ones", 0, 1), j == 0, j == 2) for i in (1, 2) for j in range(3)])
+            gfill("dw2", 0, CAP, 0)
+        act(S("ec", 0, 128), W(xc, 0, XW + HALO, "lec%d" % t, 0, 8), AF.Copy)
+        vcopy(S("eb", 0, 128), W(xc, 0, HALO + CAP, lst, 0, 8))
+        clamp(3)
+        clamp(4)
+        o = S("b1", 0, 128)
+        mms([(o, tap(t, 0), S(fl, 0, 128), True, False), (o, tap(t, 1), S("eb", 0, 128), False, False), (o, tap(t, 2), S("ec", 0, 128), False, True)])
         ts(S("er", 0, 128), S("b1", 0, 128), 0.125, bias, OP.mult, OP.add)
         ts(S("ez", 0, 64), S("er", 64, 128), OFS - 15.0, OFS + 15.0, OP.max, OP.min)
         ts(S("big", z, z + 64), S("er", 0, 64), OFS - 15.0, OFS + 15.0, OP.max, OP.min)
         vscatter(W("big", z, z + CAP, lst, 8, 12), S("ez", 0, 64))
 
-    act(S("big", V2, V2 + 1024), W("big", Z2, Z2 + 4096, "slot2", 0, 64), AF.Copy)
-    vcopy(S("big", V2 + 1024, V2 + 2048), W("big", Z2, Z2 + 4096, "slot2", 64, 128))
-    act(S("big", V1, V1 + 1024), W("big", Z1, Z1 + 4096, "slot1", 0, 64), AF.Identity, bias=-OFS)
-    ts(S("big", V1 + 1024, V1 + 2048), W("big", Z1, Z1 + 4096, "slot1", 64, 128), -OFS, None, OP.add)
-    for c in range(8):
-        o, i = S("yb", 512 * c, 512 * c + 512), W("big", 0, 6144, "slot0", 32 * c, 32 * c + 32)
-        if c % 2:
-            act(o, i, AF.Copy)
-        else:
-            vcopy(o, i)
-        emit("s", lambda: g.sync.dma_start(T.y[:, 512 * c:512 * c + 512], T.yb[:, 512 * c:512 * c + 512]),
-             [("yb", 512 * c, 512 * c + 512)], [], dma="dy%d" % c)
+    def back(level, c):
+        lo, mid, hi = 512 * c, 512 * c + 256, 512 * c + 512
+        src, top = ((0, V1), (Z1, V2), (Z2, Z3))[level]
+        for eng, a, b in (("a", lo, mid), ("v", mid, hi)):
+            i = W("big", src, top + min(hi, CAP), "slot%d" % level, a // 16, b // 16)
+            o = S("yb", a, b) if level == 0 else S("big", (0, V1, V2)[level] + a, (0, V1, V2)[level] + b)
+            if eng == "a":
+                act(o, i, AF.Copy) if level != 1 else act(o, i, AF.Identity, bias=-OFS)
+            elif level != 1:
+                vcopy(o, i)
+            else:
+                ts(o, i, -OFS, None, OP.add)
+        if level == 0:
+            emit("s", lambda: g.sync.dma_start(T.y[:, lo:hi], T.yb[:, lo:hi]), [("yb", lo, hi)], [], dma="dy%d" % c)
+
+    for level, c in ((2, 0), (1, 0), (2, 1), (0, 0), (1, 1), (2, 2), (0, 1), (1, 2), (2, 3), (0, 2), (1, 3), (0, 3), (0, 4), (0, 5), (0, 6), (0, 7)):
+        back(level, c)
     tr["finish"]()

@@ -18,7 +18,8 @@ for _t in range(3):
     for _n, _k, _d in (("xc", XW + HALO, "bfloat16"), ("fl", 2 * HALO, "bfloat16"), ("dw", DWW, "bfloat16"), ("rm", RMW, "bfloat16"),
                        ("sv", 144, "bfloat16"), ("pen", 128, "bfloat16"), ("q", 12, "float32"), ("pc", 8, "float32"),
                        ("lb", 128, "uint16"), ("lc", 128, "uint16"), ("lst", 12, "uint16"), ("lec", 8, "uint16"), ("fll", 8, "uint16"),
-                       ("off", 16, "uint16"), ("la", 64, "uint16"), ("ll", 64, "uint16"), ("slot", 128 if _t else 256, "uint16")):
+                       ("off", 16, "uint16"), ("la", 32, "uint16"), ("lm", 32, "uint16"), ("ll", 64, "uint16"),
+                       ("slot", 128 if _t else 256, "uint16")):
         _W[_d]["%s%d" % (_n, _t)] = _k
 SCRATCH = {n: ("sbuf", [128, k], d) for d, a in _W.items() for n, k in a.items()}
 SCRATCH["wb"] = ("sbuf", [128, 9, 16], "bfloat16")
@@ -170,6 +171,9 @@ def rank_program(g, core, T, topo):
     def win(name, k):
         return S(name, 15 - k, 143 - k)
 
+    def wrap(out, lhs, name, lo, hi):
+        mms([(out, win(lhs, k), S(name, lo + k, hi, 16), k == 0, k == 15) for k in range(16)])
+
     def tap(t, j):
         i = 3 * t + j
         return T.wbd[:, i, :], [("wbd", i, i + 1)]
@@ -299,11 +303,12 @@ def rank_program(g, core, T, topo):
         nw = nb // 16
         rm, dw, xc, lst, fl, sv = ["%s%d" % (n, t) for n in ("rm", "dw", "xc", "lst", "fl", "sv")]
         src0, srcn = (0, 4096) if t == 0 else (zoff[t - 1], CAP)
+        space = (src0, src0 + srcn)
         M0, R0 = 16, 16 + nb
         if t == 0:
             for c in range(4):
                 ob = S("b0", 64 * c, 64 * c + 64) if c < 3 else S("b3", 0, 64)
-                mms([(ob, win(sv, k), S("big", 1024 * c + k, 1024 * c + 1024, 16), k == 0, k == 15) for k in range(16)])
+                wrap(ob, sv, "big", 1024 * c, 1024 * c + 1024)
                 if c == 2:
                     ts(S(rm, M0, M0 + 192), S("b0", 0, 192), C(TH), None, OP.is_ge)
             ts(S(rm, M0 + 192, M0 + 256), S("b3", 0, 64), C(TH), None, OP.is_ge)
@@ -352,30 +357,40 @@ def rank_program(g, core, T, topo):
                 ts(S("cf", 0, 64), S("u", 0, 64), C(BMIN), None, OP.min)
             u0 = S("u", hi - 1, hi)
         ts(S("cf", 64, 128), W("u", 0, CAP, lst, 8, 12), C(BMIN), None, OP.min)
-        mms([(S("b2", 0, 8), win("el2", k), S("cf", k, 128, 16), k == 0, k == 15) for k in range(16)])
+        wrap(S("b1", 0, 32), "el1", "cb", 0, 512)
+        wrap(S("b2", 0, 8), "el2", "cf", 0, 128)
+        vcopy(S("la%d" % t, 0, 32), S("b1", 0, 32))
+        act(S(xc, 64, 576), W("big", *space, "la%d" % t, 0, 32), AF.Copy)
         ts(S("cb", 1024, 2048), S("u", 1024, 2048), C(BMIN), None, OP.min)
         ts(S("fll%d" % t, 0, 8), S("b2", 0, 8), 15.0, None, OP.add)
-        vcopy(S(fl, 0, 128), W("big", src0, src0 + srcn, "fll%d" % t, 0, 8))
+        vcopy(S(fl, 0, 128), W("big", *space, "fll%d" % t, 0, 8))
         send(t)
-        mms([(S("b1", 0, 64), win("el1", k), S("cb", k, 1024, 16), k == 0, k == 15) for k in range(16)])
-        mms([(S("b0", 0, 64), win("el2", k), S("cb", 1024 + k, 2048, 16), k == 0, k == 15) for k in range(16)])
-        vcopy(S("la%d" % t, 0, 64), S("b1", 0, 64))
-        act(S(xc, 64, 1088), W("big", src0, src0 + srcn, "la%d" % t, 0, 64), AF.Copy)
+        wrap(S("b1", 0, 32), "el1", "cb", 512, 1024)
+        wrap(S("b0", 0, 64), "el2", "cb", 1024, 2048)
+        ts(S("pm", 0, 8), S("pc%d" % t, 0, 8), C(KR), C(KC), OP.is_ge, OP.mult)
+        vcopy(S("lm%d" % t, 0, 32), S("b1", 0, 32))
+        act(S(xc, 576, 1088), W("big", *space, "lm%d" % t, 0, 32), AF.Copy)
+        tt(S("pm", 0, 8), S("pm", 0, 8), S("pc%d" % t, 0, 8), OP.add)
+        if t < 2:
+            ts(S("pen%d" % (t + 1), 0, 128), S("iw", 0, 128), C(KR), -32768.0, OP.is_ge, OP.mult)
+        ts(S("lec%d" % t, 0, 8), S("pm", 0, 8), 64.0, None, OP.add)
         if t:
             slots_b(t - 1)
         ts(S("ll%d" % t, 0, 64), S("b0", 0, 64), 15.0, None, OP.add)
-        vcopy(S(xc, 1088, 2112), W("big", src0, src0 + srcn, "ll%d" % t, 0, 64))
+        cut = 1728
+        vcopy(S(xc, 1088, 64 + cut), W("big", *space, "ll%d" % t, 0, cut // 16 - 64))
+        act(S(xc, 64 + cut, 2112), W("big", *space, "ll%d" % t, cut // 16 - 64, 64), AF.Copy)
         z = zoff[t]
         bias = OFS if t == 0 else C(BIAS + t)
-        ch = [(64, 512), (512, 1024), (1024, 1536), (1536, 1856), (1856, 2048)]
+        ch = [(64, 512), (512, 1024), (1024, 1536), (1536, 1920), (1920, 2048)]
 
         def left(c):
             lo, hi = ch[c]
-            vcopy(S("gb", lo, hi), W(xc, HALO, HALO + CAP, "lb%d" % t, lo // 16, hi // 16))
+            vcopy(S("gb", lo, hi), W(xc, HALO, HALO + hi, "lb%d" % t, lo // 16, hi // 16))
 
         def right(c, eng="a"):
             lo, hi = ch[c]
-            o, i = S("gc", lo, hi), W(xc, HALO, XW, "lc%d" % t, lo // 16, hi // 16)
+            o, i = S("gc", lo, hi), W(xc, HALO, 2 * HALO + hi, "lc%d" % t, lo // 16, hi // 16)
             act(o, i, AF.Copy) if eng == "a" else vcopy(o, i)
 
         def bank(c):
@@ -403,31 +418,27 @@ def rank_program(g, core, T, topo):
         near(0); left(2); right(2); mix(2)
         near(1); clamp(0); left(3); right(3); mix(3)
         left(4); right(4, "v"); mix(4)
-        near(2); near(3)
-        ts(S("pm", 0, 8), S("pc%d" % t, 0, 8), C(KR), C(KC), OP.is_ge, OP.mult)
+        near(2)
         clamp(1)
-        tt(S("pm", 0, 8), S("pm", 0, 8), S("pc%d" % t, 0, 8), OP.add)
-        if t < 2:
-            ts(S("pen%d" % (t + 1), 0, 128), S("iw", 0, 128), C(KR), -32768.0, OP.is_ge, OP.mult)
-        ts(S("lec%d" % t, 0, 8), S("pm", 0, 8), 64.0, None, OP.add)
         if t == 2:
             slots_a(2)
             slots_b(2)
-        near(4, "v")
-        clamp(2)
         if t == 0:
             mms([(S("b2", 8, 11), S("bd", 0, 128), S("vb", 0, 3), True, True)]
                 + [(S("b2", 8 + 4 * i, 9 + 4 * i), tap(i, j), S("ones", 0, 1), j == 0, j == 2) for i in (1, 2) for j in range(3)])
             gfill("dw2", 0, CAP, 0)
         act(S("ec", 0, 128), W(xc, 0, XW + HALO, "lec%d" % t, 0, 8), AF.Copy)
         vcopy(S("eb", 0, 128), W(xc, 0, HALO + CAP, lst, 0, 8))
-        clamp(3)
-        clamp(4)
         o = S("b1", 0, 128)
         mms([(o, tap(t, 0), S(fl, 0, 128), True, False), (o, tap(t, 1), S("eb", 0, 128), False, False), (o, tap(t, 2), S("ec", 0, 128), False, True)])
+        near(3)
+        near(4, "v")
+        clamp(2)
         ts(S("er", 0, 128), S("b1", 0, 128), 0.125, bias, OP.mult, OP.add)
+        clamp(3)
         ts(S("ez", 0, 64), S("er", 64, 128), OFS - 15.0, OFS + 15.0, OP.max, OP.min)
         ts(S("big", z, z + 64), S("er", 0, 64), OFS - 15.0, OFS + 15.0, OP.max, OP.min)
+        clamp(4)
         vscatter(W("big", z, z + CAP, lst, 8, 12), S("ez", 0, 64))
 
     def back(level, c):

@@ -4,20 +4,22 @@ from concourse.mybir import AluOpType, ActivationFunctionType
 OP = AluOpType
 AF = ActivationFunctionType
 CAP, HALO, OFS = 2048, 64, 192.0
-XW = HALO + CAP + HALO
+XW = HALO + CAP
 V1, Z1, V2, Z2, Z3, BIGW = 4096, 6144, 8192, 10240, 12288, 14336
-DWW, RMW = CAP + 256, 544
+DWW, RMW = CAP + 256, 576
+PARTS = [(0, 512), (512, 1024), (1024, 1536), (1536, 1920), (1920, 2048)]
+CUT = 1728
 
-_W = {"bfloat16": {"big": BIGW, "gb": CAP, "gc": CAP, "zr": CAP, "u": CAP, "cb": CAP, "dc": CAP, "dsb": 256, "mrow": 256,
-                   "e": 144, "bd": 128, "idn": 128, "idk": 128, "ltf": 128, "lt": 128, "s15": 128, "el1": 144, "el2": 144,
-                   "chi": 16, "clo": 16, "ones": 16, "vb": 3, "eb": 128, "ec": 128, "er": 128, "ez": 64, "cf": 128},
+_W = {"bfloat16": {"big": BIGW, "gb": CAP, "gc": CAP, "u": CAP, "cb": CAP, "dc": CAP, "dsb": 256, "mrow": 256,
+                   "e": 144, "bd": 128, "idn": 128, "idk": 128, "idb": 128, "ltf": 128, "lt": 128, "s15": 128, "el1": 144, "el2": 144,
+                   "chi": 16, "clo": 16, "ones": 512, "vb": 3, "cf": 128},
       "float32": {"yb": 4096, "jrow": 144, "jg": 128, "ir": 256, "iw": 256, "own0": 256, "own1": 128, "m16": 16, "g8": 8, "gm": 8,
-                  "cc": 64, "tmp3": 3, "of1": 16, "of2": 16, "st": 256, "pm": 8, "qr": 12},
+                  "cc": 64, "of1": 16, "of2": 16, "st": 256, "qk": 4, "lcf": 128},
       "int32": {"ip": 1, "gi": 1, "ki": 1, "thi": 3, "gpi": 3}, "uint16": {}}
 for _t in range(3):
     for _n, _k, _d in (("xc", XW + HALO, "bfloat16"), ("fl", 2 * HALO, "bfloat16"), ("dw", DWW, "bfloat16"), ("rm", RMW, "bfloat16"),
-                       ("sv", 144, "bfloat16"), ("pen", 128, "bfloat16"), ("q", 12, "float32"), ("pc", 8, "float32"),
-                       ("lb", 128, "uint16"), ("lc", 128, "uint16"), ("lst", 12, "uint16"), ("lec", 8, "uint16"), ("fll", 8, "uint16"),
+                       ("sv", 144, "bfloat16"), ("pen", 128, "bfloat16"), ("iwd", 128, "float32"),
+                       ("lb", 128, "uint16"), ("lc", 128, "uint16"), ("lst", 8, "uint16"), ("fll", 8, "uint16"),
                        ("off", 16, "uint16"), ("la", 32, "uint16"), ("lm", 32, "uint16"), ("ll", 64, "uint16"),
                        ("slot", 128 if _t else 256, "uint16")):
         _W[_d]["%s%d" % (_n, _t)] = _k
@@ -28,9 +30,9 @@ BANKS = ["b%d" % i for i in range(8)]
 for _b in BANKS:
     SCRATCH[_b] = ("psum", [128, 512], "float32")
 SEMAPHORES = (["cv", "ca", "cp", "cg", "dv", "dt", "dg", "dwt", "sent"] + ["dx%d" % i for i in range(4)]
-              + ["dy%d" % i for i in range(8)] + ["al%d" % i for i in range(3)] + ["ar%d" % i for i in range(3)])
+              + ["dy%d" % i for i in range(16)] + ["al%d" % i for i in range(3)] + ["ar%d" % i for i in range(3)])
 PF, GF, KF, G15, K15, ND, SC, BI, BMIN, WL1, WL2, KLO = range(12)
-TH, GAP, BIAS, G16, VF, NG, KC, KR = 12, 15, 18, 21, 22, 25, 28, 29
+TH, GAP, G16, VF, KC, KR = 12, 15, 21, 22, 28, 29
 
 
 def tracker(g, T):
@@ -194,15 +196,15 @@ def rank_program(g, core, T, topo):
     iota("g8", 0, 8, [[1, 8]], 0, 0)
     for t in range(3):
         gfill("rm%d" % t, 0, 16, 0)
+    gfill("rm0", 288, 304, 0)
+    gfill("dw0", 1024, CAP, 0)
     for t in range(3):
-        gfill("xc%d" % t, HALO + CAP, XW, 0)
-        zero = 0 if t == 0 else int(OFS)
         if rank == 0:
-            gfill("xc%d" % t, 0, HALO, zero)
+            gfill("xc%d" % t, 0, HALO, 0)
         if rank == nranks - 1:
-            gfill("xc%d" % t, XW, XW + HALO, zero)
+            gfill("xc%d" % t, XW, XW + HALO, 0)
+    gfill("ones", 0, 512, 1)
     gfill("dw1", 0, CAP, 0)
-    vfill(S("ones", 0, 16), 1.0)
     ts(S("gi", 0, 1), S("ip", 0, 1), 4, None, OP.logical_shift_right)
     ts(S("ki", 0, 1), S("ip", 0, 1), 15, None, OP.bitwise_and)
     vcopy(C(PF), S("ip", 0, 1))
@@ -211,49 +213,50 @@ def rank_program(g, core, T, topo):
     ts(C(G15), C(GF), 16.0, 15.0, OP.mult, OP.add)
     ts(C(K15), C(KF), 15.0, None, OP.is_equal)
     ts(S("e", 0, 144), S("jrow", 0, 144), C(G15), None, OP.is_equal)
-    vfill(S("dw0", 0, CAP), 0.0)
     ts(S("sv0", 0, 144), S("e", 0, 144), S("vb", 0, 1), None, OP.mult)
     for col, sc, bi in ((ND, 1.0, -1.0), (SC, 2.0, -1.0), (BI, -1.0, 1.0), (BMIN, 255.0, 1.0), (WL1, 15.0, 1.0), (WL2, 17.0, -1.0)):
         act(C(col), C(K15), AF.Identity, bias=bi, scale=sc)
     act(C(G16), C(GF), AF.Copy, scale=-16.0)
     act(C(KLO), C(KF), AF.Copy, scale=-1.0 / 8192)
-    act(S("dc", 0, CAP), S("dw0", 0, CAP), AF.Identity, bias=C(ND))
     ts(S("bd", 0, 128), S("jg", 0, 128), C(GF), None, OP.is_equal)
     ts(S("ltf", 0, 128), S("jrow", 0, 128), C(PF), None, OP.is_ge)
     ts(S("idn", 0, 128), S("jrow", 0, 128), C(PF), None, OP.is_equal)
     tt(S("ltf", 0, 128), S("ltf", 0, 128), S("bd", 0, 128), OP.mult)
     ts(S("s15", 0, 128), S("idn", 0, 128), C(K15), None, OP.mult)
     tt(S("lt", 0, 128), S("ltf", 0, 128), S("e", 0, 128), OP.subtract)
-    ts(S("idk", 0, 128), S("idn", 0, 128), 8192.0, None, OP.mult)
-    ts(S("gm", 0, 8), S("g8", 0, 8), C(GF), None, OP.is_equal)
     vcopy(S("cc", TH, TH + 3), S("thi", 0, 3))
+    vfill(S("dw0", 0, 1024), 0.0)
     vcopy(S("cc", GAP, GAP + 3), S("gpi", 0, 3))
     vcopy(S("cc", VF, VF + 3), S("vb", 0, 3))
-    ts(S("cc", NG, NG + 3), S("cc", GAP, GAP + 3), -1.0, None, OP.mult)
     ts(S("iw", 0, 256), S("ir", 0, 256), C(G16), None, OP.add)
     ts(S("chi", 0, 16), S("m16", 0, 16), 2048.0, -1.0 / 8192, OP.add, OP.mult)
     ts(S("clo", 0, 16), S("m16", 0, 16), 0.0, C(KLO), OP.mult, OP.add)
-    act(S("el1", 0, 144), S("e", 0, 144), AF.Copy, scale=C(WL1))
-    act(S("el2", 0, 144), S("e", 0, 144), AF.Copy, scale=C(WL2))
+    for lo in (0, 1024):
+        act(S("dc", lo, lo + 1024), S("big", 0, 1024), AF.Identity, bias=C(ND), scale=0.0)
     for t in (1, 2):
         act(S("sv%d" % t, 0, 144), S("e", 0, 144), AF.Copy, scale=C(VF + t))
-    for t in range(3):
-        iw4, q = S("iw", 0, 4), "q%d" % t
-        act(S(q, 4, 8), iw4, AF.Identity, bias=C(NG + t))
-        act(S(q, 8, 12), iw4, AF.Identity, bias=-64.0)
-        act(S("pc%d" % t, 0, 4), iw4, AF.Identity, bias=C(GAP + t))
-        act(S("qr", 4 * t, 4 * t + 4), S(q, 8, 12), AF.Identity, bias=C(GAP + t))
+    ts(S("gm", 0, 8), S("g8", 0, 8), C(GF), 0.125, OP.is_equal, OP.mult)
+    act(S("iwd0", 0, 128), S("iw", 0, 128), AF.Identity, bias=C(GAP))
+    act(S("qk", 0, 4), S("iw", 0, 4), AF.Identity, bias=-64.0)
+    act(S("el1", 0, 144), S("e", 0, 144), AF.Copy, scale=C(WL1))
+    act(S("el2", 0, 144), S("e", 0, 144), AF.Copy, scale=C(WL2))
     base = [4096 - 1 - 8192, 2048 - 1 - 8192]
-    for i, n in ((0, 256), (1, 128)):
-        act(S("own%d" % i, 0, n), S("iw", 0, n), AF.Identity, bias=float(-base[i]))
-    for i in range(8):
-        emit("a", lambda: g.scalar.activation(T.wbd[:, :, 16 * i:16 * i + 16], T.wb[:, :, :], AF.Copy, scale=T.gm[:, i:i + 1]),
-             [("wb", 0, 9), ("gm", i, i + 1)], [("wbd", 0, 9)] if i == 7 else [])
+
+    def tap_matrices(first, last):
+        for i in range(first, last):
+            emit("a", lambda: g.scalar.activation(T.wbd[:, :, 16 * i:16 * i + 16], T.wb[:, :, :], AF.Copy, scale=T.gm[:, i:i + 1]),
+                 [("wb", 0, 9), ("gm", i, i + 1)], [("wbd", 0, 9)] if i == 7 else [])
+
+    def later_constants():
+        for i, n in ((0, 256), (1, 128)):
+            act(S("own%d" % i, 0, n), S("iw", 0, n), AF.Identity, bias=float(-base[i]))
+        for t in (1, 2):
+            act(S("iwd%d" % t, 0, 128), S("iw", 0, 128), AF.Identity, bias=C(GAP + t))
+            act(C(TH + t), S("b3", 300 + t, 301 + t), AF.Identity, bias=C(TH + t), scale=OFS)
 
     def shift_lists(t):
         ts(S("lst%d" % t, 0, 4), S("iw", 0, 4), C(GAP + t), 64.0, OP.subtract, OP.add)
         ts(S("lb%d" % t, 4, 128), S("iw", 4, 128), C(GAP + t), None, OP.subtract)
-        ts(S("lc%d" % t, 4, 128), S("iw", 4, 128), C(GAP + t), None, OP.add)
 
     def slots_a(t):
         n = 128 if t else 256
@@ -298,164 +301,204 @@ def rank_program(g, core, T, topo):
                 en = len(topo.engines(T.cores[peer], core))
                 tr["landing"](key, en if peer in (0, nranks - 1) else en // 2, [("xc%d" % t, lo, lo + HALO)])
 
+    def scores(t, half):
+        ob = S("b0", 0, 64) if half == 0 else S("b2", 0, 64)
+        c0, s0 = 64 * half, zoff[t - 1] + 1024 * half
+        mms([(ob, S("idn", 0, 128), S("pen%d" % t, c0, c0 + 64), True, False)]
+            + [(ob, win("sv%d" % t, k), S("big", s0 + k, s0 + 1024, 16), False, k == 15) for k in range(16)])
+
+    def back(eng, level, lo, hi):
+        src, top = ((0, V1), (Z1, V2), (Z2, Z3))[level]
+        i = W("big", src, top + min(hi, CAP), "slot%d" % level, lo // 16, hi // 16)
+        o = S("yb", lo, hi) if level == 0 else S("big", (0, V1, V2)[level] + lo, (0, V1, V2)[level] + hi)
+        if eng == "a":
+            act(o, i, AF.Copy) if level != 1 else act(o, i, AF.Identity, bias=-OFS)
+        elif level != 1:
+            vcopy(o, i)
+        else:
+            ts(o, i, -OFS, None, OP.add)
+
+    def store(lo, hi):
+        emit("s", lambda: g.sync.dma_start(T.y[:, lo:hi], T.yb[:, lo:hi]), [("yb", lo, hi)], [], dma="dy%d" % (lo // 256))
+
     for t in range(3):
-        nb = 256 if t == 0 else 128
-        nw = nb // 16
         rm, dw, xc, lst, fl, sv = ["%s%d" % (n, t) for n in ("rm", "dw", "xc", "lst", "fl", "sv")]
-        src0, srcn = (0, 4096) if t == 0 else (zoff[t - 1], CAP)
-        space = (src0, src0 + srcn)
-        M0, R0 = 16, 16 + nb
+        space = (0, 4096) if t == 0 else (zoff[t - 1], zoff[t - 1] + CAP)
+        z = zoff[t]
+        P0 = (16, 304) if t == 0 else (16,)
+        last = len(P0) - 1
+
+        def mark(p):
+            m0, r0, c0, w0, o = P0[p], P0[p] + 128, 128 * p, 8 * p, 32 * p
+            mms([(S("b1", c0, c0 + 128), S("lt", 0, 128), S(rm, m0, r0), True, False),
+                 (S("b1", c0, c0 + 128), S("s15", 0, 128), S("mrow", c0, c0 + 128), False, True)])
+            scan(S(rm, r0, r0 + 129), S(rm, m0 - 1, r0), S(rm, m0 - 1, r0), S(rm, P0[0] + 256, P0[0] + 257) if p else 0.0, OP.add, OP.max)
+            act(S("dsb", c0, c0 + 128), S("b1", c0, c0 + 128), AF.Copy)
+            if p == last:
+                mms([(S("b3", 0, 1), S("bd", 0, 128), S(rm, r0 + 128, r0 + 129), True, True)])
+            b2, b2m = S("b2", o, o + 16), S("b2", o, o + 8)
+            rhs = [(win("e", k), S(rm, m0 + k, m0 + 256, 16)) for k in range(16)]
+            mms([(b2, rhs[0][0], rhs[0][1], True, False),
+                 (b2m, S("idn", 0, 128), S("chi", w0, w0 + 8), False, False), (b2m, S("idn", 0, 128), S("clo", w0, w0 + 8), False, False)]
+                + [(b2, rhs[k][0], rhs[k][1], False, k == 15) for k in range(1, 16)])
+
+        def offsets(p, fill1=None, fill2=None):
+            w0, o = 8 * p, 32 * p
+            ts(S("of1", w0, w0 + 8), S("b2", o, o + 8), -8192.0, None, OP.mult)
+            if fill1:
+                fill1()
+            tt(S("of2", w0, w0 + 8), S("of1", w0, w0 + 8), S("b2", o + 8, o + 16), OP.max)
+            if fill2:
+                fill2()
+            vcopy(S("off%d" % t, w0, w0 + 8), S("of2", w0, w0 + 8))
+
+        def scatter(p):
+            vscatter(W(dw, 0, DWW, "off%d" % t, 8 * p, 8 * p + 8), S("dsb", 128 * p, 128 * p + 128))
+
+        def pick(eng, out, lname, l0, l1):
+            i = W("big", *space, lname, l0, l1)
+            if eng == "a":
+                act(out, i, AF.Copy) if t == 0 else act(out, i, AF.Identity, bias=-OFS)
+            else:
+                vcopy(out, i) if t == 0 else ts(out, i, -OFS, None, OP.add)
+
+        def left(eng, lo, hi):
+            o, i = S("gb", lo, hi), W(xc, HALO, HALO + hi, "lb%d" % t, lo // 16, hi // 16)
+            act(o, i, AF.Copy) if eng == "a" else vcopy(o, i)
+
+        def right(eng, lo, hi):
+            o, i = S("gc", lo, hi), W(xc, HALO, XW + HALO, "lc%d" % t, lo // 16, hi // 16)
+            act(o, i, AF.Copy) if eng == "a" else vcopy(o, i)
+
+        def bank(c):
+            return S(("b4", "b5", "b6", "b7", "b1")[c], 0, PARTS[c][1] - PARTS[c][0])
+
+        def offset(c):
+            mms([(bank(c), S("idb", 0, 128), S("ones", 0, PARTS[c][1] - PARTS[c][0]), True, False)])
+
+        def mix(c, j):
+            lo, hi = PARTS[c]
+            mms([(bank(c), tap(t, j), S(*((xc, HALO + lo, HALO + hi), ("gb", lo, hi), ("gc", lo, hi))[j]), False, j == 2)])
+
+        def near(c):
+            lo, hi = PARTS[c]
+            ts(S("big", z + lo, z + hi), bank(c), OFS - 15.0, OFS + 15.0, OP.max, OP.min)
+
         if t == 0:
             for c in range(4):
-                ob = S("b0", 64 * c, 64 * c + 64) if c < 3 else S("b3", 0, 64)
-                wrap(ob, sv, "big", 1024 * c, 1024 * c + 1024)
+                wrap(S("b0" if c < 2 else "b3", 64 * (c % 2), 64 * (c % 2) + 64), sv, "big", 1024 * c, 1024 * c + 1024)
+                if c == 1:
+                    ts(S(rm, 16, 144), S("b0", 0, 128), C(TH), None, OP.is_ge)
                 if c == 2:
-                    ts(S(rm, M0, M0 + 192), S("b0", 0, 192), C(TH), None, OP.is_ge)
-            ts(S(rm, M0 + 192, M0 + 256), S("b3", 0, 64), C(TH), None, OP.is_ge)
-        else:
-            mms([(S("b0", 0, nb), S("idn", 0, 128), S("pen%d" % t, 0, 128), True, False)]
-                + [(S("b0", 0, nb), win(sv, k), S("big", src0 + k, src0 + CAP, 16), False, k == 15) for k in range(16)])
-            if t == 1:
-                ts(S("tmp3", 1, 3), S("b2", 9, 11), OFS, None, OP.mult)
-                tt(S("cc", TH + 1, TH + 3), S("cc", TH + 1, TH + 3), S("tmp3", 1, 3), OP.add)
-                for i in (1, 2):
-                    ts(C(BIAS + i), S("b2", 8 + 4 * i, 9 + 4 * i), -24.0, OFS, OP.mult, OP.add)
-            shift_lists(t)
-            ts(S(rm, M0, M0 + nb), S("b0", 0, nb), C(TH + t), None, OP.is_ge)
-        mms([(S("b1", 0, nb), S("lt", 0, 128), S(rm, M0, M0 + nb), True, False),
-             (S("b1", 0, nb), S("s15", 0, 128), S("mrow", 0, nb), False, True)])
-        scan(S(rm, R0, R0 + nb + 1), S(rm, M0 - 1, M0 + nb), S(rm, M0 - 1, M0 + nb), 0.0, OP.add, OP.max)
-        act(S("dsb", 0, nb), S("b1", 0, nb), AF.Copy)
-        if t == 0:
+                    tap_matrices(0, 2)
+                    mark(0)
             shift_lists(0)
+            for name, c in (("idk", 8192.0), ("idb", OFS)):
+                ts(S(name, 0, 128), S("idn", 0, 128), c, None, OP.mult)
+            offsets(0)
+            ts(S(rm, 304, 432), S("b3", 0, 128), C(TH), None, OP.is_ge)
         else:
+            scores(t, 1)
+            shift_lists(t)
             slots_a(t - 1)
-        b2 = S("b2", 0, 2 * nw)
-        rhs = [(win("e", k), S(rm, M0 + k, M0 + 2 * nb, 16)) for k in range(16)]
-        mms([(b2, rhs[0][0], rhs[0][1], True, False),
-             (S("b2", 0, nw), S("idn", 0, 128), S("chi", 0, nw), False, False), (S("b2", 0, nw), S("idn", 0, 128), S("clo", 0, nw), False, False)]
-            + [(b2, rhs[k][0], rhs[k][1], False, k == 15) for k in range(1, 16)])
-        mms([(S("b3", 0, 1), S("bd", 0, 128), S(rm, R0 + nb, R0 + nb + 1), True, True)])
-        ts(S("of1", 0, nw), S("b2", 0, nw), -8192.0, None, OP.mult)
-        tt(S("of2", 0, nw), S("of1", 0, nw), S("b2", nw, 2 * nw), OP.max)
-        vcopy(S("off%d" % t, 0, nw), S("of2", 0, nw))
-        vscatter(W(dw, 0, DWW, "off%d" % t, 0, nw), S("dsb", 0, nb))
+            ts(S(rm, 16, 80), S("b0", 0, 64), C(TH + t), None, OP.is_ge)
+            ts(S(rm, 80, 144), S("b2", 0, 64), C(TH + t), None, OP.is_ge)
+        mark(last)
+        if t == 0:
+            scatter(0)
+        else:
+            slots_b(t - 1)
         act(C(KR), S("b3", 0, 1), AF.Copy)
-        act(C(KC), C(KR), AF.Identity, bias=float(XW - HALO), scale=-1.0)
-        act(S("pc%d" % t, 4, 8), S("qr", 4 * t, 4 * t + 4), AF.Identity, bias=C(KR))
-        cum = S("b3", 16, 16 + nb)
-        mms([(cum, S("bd", 0, 128), S(rm, R0, R0 + nb), True, False), (cum, S("ltf", 0, 128), S(rm, M0, M0 + nb), False, False),
-             (cum, S("idk", 0, 128), S(rm, M0, M0 + nb), False, True)])
+        act(C(KC), S("b3", 0, 1), AF.Copy, bias=float(XW - HALO), scale=-1.0)
+        lcsel = S("b0", 256, 384)
+        offsets(last, lambda: ts(lcsel, S("iwd%d" % t, 0, 128), C(KR), C(KC), OP.is_ge, OP.mult),
+                lambda: ts(S(lst, 4, 8), S("qk", 0, 4), C(KR), None, OP.add))
+        scatter(last)
+        for p in range(last + 1):
+            cum, m0 = S("b3", 16 + 128 * p, 144 + 128 * p), P0[p]
+            mms([(cum, S("bd", 0, 128), S(rm, m0 + 128, m0 + 256), True, False), (cum, S("ltf", 0, 128), S(rm, m0, m0 + 128), False, False),
+                 (cum, S("idk", 0, 128), S(rm, m0, m0 + 128), False, True)])
+        if t == 0:
+            tap_matrices(2, 8)
+            mms([(S("b3", 300, 303), S("bd", 0, 128), S("vb", 0, 3), True, True)])
         u0 = 0.0
         for lo, hi in ((0, 512), (512, 1024), (1024, 2048)):
             scan(S("u", lo, hi), S("dc", lo, hi), S(dw, lo, hi), u0, OP.add, OP.max)
             if lo < 1024:
                 act(S("cb", lo, hi), S("u", lo, hi), AF.Relu, bias=C(BI), scale=C(SC))
             if lo == 0:
-                ts(S(lst, 4, 12), S("q%d" % t, 4, 12), C(KR), None, OP.add)
+                tt(S("lcf", 0, 128), S("iwd%d" % t, 0, 128), lcsel, OP.add)
             if lo == 512:
                 ts(S("cf", 0, 64), S("u", 0, 64), C(BMIN), None, OP.min)
+            if lo == 1024:
+                ts(S("lc%d" % t, 0, 128), S("lcf", 0, 128), float(CAP + HALO - 1), None, OP.min)
             u0 = S("u", hi - 1, hi)
-        ts(S("cf", 64, 128), W("u", 0, CAP, lst, 8, 12), C(BMIN), None, OP.min)
+        ts(S("cf", 64, 128), W("u", 0, CAP, lst, 4, 8), C(BMIN), None, OP.min)
+        for c in range(3):
+            offset(c)
         wrap(S("b1", 0, 32), "el1", "cb", 0, 512)
         wrap(S("b2", 0, 8), "el2", "cf", 0, 128)
         vcopy(S("la%d" % t, 0, 32), S("b1", 0, 32))
-        act(S(xc, 64, 576), W("big", *space, "la%d" % t, 0, 32), AF.Copy)
+        pick("a", S(xc, 64, 576), "la%d" % t, 0, 32)
         ts(S("cb", 1024, 2048), S("u", 1024, 2048), C(BMIN), None, OP.min)
         ts(S("fll%d" % t, 0, 8), S("b2", 0, 8), 15.0, None, OP.add)
-        vcopy(S(fl, 0, 128), W("big", *space, "fll%d" % t, 0, 8))
+        pick("v", S(fl, 0, 128), "fll%d" % t, 0, 8)
         send(t)
         wrap(S("b1", 0, 32), "el1", "cb", 512, 1024)
         wrap(S("b0", 0, 64), "el2", "cb", 1024, 2048)
-        ts(S("pm", 0, 8), S("pc%d" % t, 0, 8), C(KR), C(KC), OP.is_ge, OP.mult)
         vcopy(S("lm%d" % t, 0, 32), S("b1", 0, 32))
-        act(S(xc, 576, 1088), W("big", *space, "lm%d" % t, 0, 32), AF.Copy)
-        tt(S("pm", 0, 8), S("pm", 0, 8), S("pc%d" % t, 0, 8), OP.add)
+        pick("a", S(xc, 576, 1088), "lm%d" % t, 0, 32)
+        ts(S("ll%d" % t, 0, 64), S("b0", 0, 64), 15.0, None, OP.add)
+        pick("v", S(xc, 1088, 64 + CUT), "ll%d" % t, 0, CUT // 16 - 64)
+        pick("a", S(xc, 64 + CUT, 2112), "ll%d" % t, CUT // 16 - 64, 64)
+        offset(3)
+        offset(4)
+        left("a", 64, 512)
+        left("v", 1024, 1536)
+        left("a", 512, 1024)
+        left("v", 1536, 2048)
+        for c in range(5):
+            mix(c, 0)
+        vcopy(S("gb", 0, 64), W(xc, 0, HALO + 64, lst, 0, 4))
+        right("a", 0, 512)
+        for c in (2, 1, 3, 4, 0):
+            mix(c, 1)
+        right("v", 1536, 1920)
+        mix(0, 2)
+        right("a", 512, 1024)
+        mix(3, 2)
+        right("a", 1024, 1536)
+        mix(1, 2)
         if t < 2:
             ts(S("pen%d" % (t + 1), 0, 128), S("iw", 0, 128), C(KR), -32768.0, OP.is_ge, OP.mult)
-        ts(S("lec%d" % t, 0, 8), S("pm", 0, 8), 64.0, None, OP.add)
-        if t:
-            slots_b(t - 1)
-        ts(S("ll%d" % t, 0, 64), S("b0", 0, 64), 15.0, None, OP.add)
-        cut = 1728
-        vcopy(S(xc, 1088, 64 + cut), W("big", *space, "ll%d" % t, 0, cut // 16 - 64))
-        act(S(xc, 64 + cut, 2112), W("big", *space, "ll%d" % t, cut // 16 - 64, 64), AF.Copy)
-        z = zoff[t]
-        bias = OFS if t == 0 else C(BIAS + t)
-        ch = [(64, 512), (512, 1024), (1024, 1536), (1536, 1920), (1920, 2048)]
-
-        def left(c):
-            lo, hi = ch[c]
-            vcopy(S("gb", lo, hi), W(xc, HALO, HALO + hi, "lb%d" % t, lo // 16, hi // 16))
-
-        def right(c, eng="a"):
-            lo, hi = ch[c]
-            o, i = S("gc", lo, hi), W(xc, HALO, 2 * HALO + hi, "lc%d" % t, lo // 16, hi // 16)
-            act(o, i, AF.Copy) if eng == "a" else vcopy(o, i)
-
-        def bank(c):
-            return S("b%d" % (4 + c % 4), 0, ch[c][1] - ch[c][0])
-
-        def mix(c):
-            lo, hi = ch[c]
-            mms([(bank(c), tap(t, 0), S(xc, HALO + lo, HALO + hi), True, False)])
-            mms([(bank(c), tap(t, 1), S("gb", lo, hi), False, False)])
-            mms([(bank(c), tap(t, 2), S("gc", lo, hi), False, True)])
-
-        def near(c, eng="a"):
-            lo, hi = ch[c]
-            if eng == "a":
-                act(S("zr", lo, hi), bank(c), AF.Identity, bias=bias, scale=0.125)
-            else:
-                ts(S("zr", lo, hi), bank(c), 0.125, bias, OP.mult, OP.add)
-
-        def clamp(c):
-            lo, hi = ch[c]
-            ts(S("big", z + lo, z + hi), S("zr", lo, hi), OFS - 15.0, OFS + 15.0, OP.max, OP.min)
-
-        right(0); left(0); mix(0)
-        right(1); left(1); mix(1)
-        near(0); left(2); right(2); mix(2)
-        near(1); clamp(0); left(3); right(3); mix(3)
-        left(4); right(4, "v"); mix(4)
-        near(2)
-        clamp(1)
-        if t == 2:
+        else:
             slots_a(2)
-            slots_b(2)
+        right("a", 1920, 2048)
         if t == 0:
-            mms([(S("b2", 8, 11), S("bd", 0, 128), S("vb", 0, 3), True, True)]
-                + [(S("b2", 8 + 4 * i, 9 + 4 * i), tap(i, j), S("ones", 0, 1), j == 0, j == 2) for i in (1, 2) for j in range(3)])
-            gfill("dw2", 0, CAP, 0)
-        act(S("ec", 0, 128), W(xc, 0, XW + HALO, "lec%d" % t, 0, 8), AF.Copy)
-        vcopy(S("eb", 0, 128), W(xc, 0, HALO + CAP, lst, 0, 8))
-        o = S("b1", 0, 128)
-        mms([(o, tap(t, 0), S(fl, 0, 128), True, False), (o, tap(t, 1), S("eb", 0, 128), False, False), (o, tap(t, 2), S("ec", 0, 128), False, True)])
+            later_constants()
+        mix(2, 2)
+        mix(4, 2)
+        if t == 2:
+            slots_b(2)
+        near(0)
+        if t == 2:
+            back("a", 2, 0, 512)
         near(3)
-        near(4, "v")
-        clamp(2)
-        ts(S("er", 0, 128), S("b1", 0, 128), 0.125, bias, OP.mult, OP.add)
-        clamp(3)
-        ts(S("ez", 0, 64), S("er", 64, 128), OFS - 15.0, OFS + 15.0, OP.max, OP.min)
-        ts(S("big", z, z + 64), S("er", 0, 64), OFS - 15.0, OFS + 15.0, OP.max, OP.min)
-        clamp(4)
-        vscatter(W("big", z, z + CAP, lst, 8, 12), S("ez", 0, 64))
+        near(1)
+        if t == 2:
+            back("a", 1, 0, 512)
+        if t < 2:
+            scores(t + 1, 0)
+        near(2)
+        near(4)
+        if t == 0:
+            gfill("dw2", 0, CAP, 0)
 
-    def back(level, c):
-        lo, mid, hi = 512 * c, 512 * c + 256, 512 * c + 512
-        src, top = ((0, V1), (Z1, V2), (Z2, Z3))[level]
-        for eng, a, b in (("a", lo, mid), ("v", mid, hi)):
-            i = W("big", src, top + min(hi, CAP), "slot%d" % level, a // 16, b // 16)
-            o = S("yb", a, b) if level == 0 else S("big", (0, V1, V2)[level] + a, (0, V1, V2)[level] + b)
-            if eng == "a":
-                act(o, i, AF.Copy) if level != 1 else act(o, i, AF.Identity, bias=-OFS)
-            elif level != 1:
-                vcopy(o, i)
-            else:
-                ts(o, i, -OFS, None, OP.add)
-        if level == 0:
-            emit("s", lambda: g.sync.dma_start(T.y[:, lo:hi], T.yb[:, lo:hi]), [("yb", lo, hi)], [], dma="dy%d" % c)
-
-    for level, c in ((2, 0), (1, 0), (2, 1), (0, 0), (1, 1), (2, 2), (0, 1), (1, 2), (2, 3), (0, 2), (1, 3), (0, 3), (0, 4), (0, 5), (0, 6), (0, 7)):
-        back(level, c)
+    for level, c in ((2, 1), (0, 0), (1, 1), (2, 2), (0, 1), (1, 2), (2, 3), (0, 2), (1, 3), (0, 3), (0, 4), (0, 5), (0, 6), (0, 7)):
+        for lo, hi in ((512 * c, 512 * c + 512),) if (level, c) != (0, 7) else ((3584, 3840), (3840, 4096)):
+            mid = (lo + hi) // 2
+            back("a", level, lo, mid)
+            back("v", level, mid, hi)
+            if level == 0:
+                store(lo, hi)
     tr["finish"]()

from concourse.bass import DstId, RemoteDMATransfer
from concourse.mybir import AluOpType, ActivationFunctionType

OP = AluOpType
AF = ActivationFunctionType
CAP, HALO, OFS = 2048, 64, 192.0
XW = HALO + CAP
V1, Z1, V2, Z2, Z3, BIGW = 4096, 6144, 8192, 10240, 12288, 14336
DWW, RMW = CAP + 256, 576
PARTS = [(0, 512), (512, 1024), (1024, 1536), (1536, 1920), (1920, 2048)]
CUT = 1728

_W = {"bfloat16": {"big": BIGW, "gb": CAP, "gc": CAP, "u": CAP, "cb": CAP, "dc": CAP, "dsb": 256, "mrow": 256,
                   "e": 144, "bd": 128, "idn": 128, "idk": 128, "idb": 128, "ltf": 128, "lt": 128, "s15": 128, "el1": 144, "el2": 144,
                   "chi": 16, "clo": 16, "ones": 512, "vb": 3, "cf": 128},
      "float32": {"yb": 4096, "jrow": 144, "jg": 128, "ir": 256, "iw": 256, "own0": 256, "own1": 128, "m16": 16, "g8": 8, "gm": 8,
                  "cc": 64, "of1": 16, "of2": 16, "st": 256, "qk": 4, "lcf": 128},
      "int32": {"ip": 1, "gi": 1, "ki": 1, "thi": 3, "gpi": 3}, "uint16": {}}
for _t in range(3):
    for _n, _k, _d in (("xc", XW + HALO, "bfloat16"), ("fl", 2 * HALO, "bfloat16"), ("dw", DWW, "bfloat16"), ("rm", RMW, "bfloat16"),
                       ("sv", 144, "bfloat16"), ("pen", 128, "bfloat16"), ("iwd", 128, "float32"),
                       ("lb", 128, "uint16"), ("lc", 128, "uint16"), ("lst", 8, "uint16"), ("fll", 8, "uint16"),
                       ("off", 16, "uint16"), ("la", 32, "uint16"), ("lm", 32, "uint16"), ("ll", 64, "uint16"),
                       ("slot", 128 if _t else 256, "uint16")):
        _W[_d]["%s%d" % (_n, _t)] = _k
SCRATCH = {n: ("sbuf", [128, k], d) for d, a in _W.items() for n, k in a.items()}
SCRATCH["wb"] = ("sbuf", [128, 9, 16], "bfloat16")
SCRATCH["wbd"] = ("sbuf", [128, 9, 128], "bfloat16")
BANKS = ["b%d" % i for i in range(8)]
for _b in BANKS:
    SCRATCH[_b] = ("psum", [128, 512], "float32")
SEMAPHORES = (["cv", "ca", "cp", "cg", "dv", "dt", "dg", "dwt", "sent"] + ["dx%d" % i for i in range(4)]
              + ["dy%d" % i for i in range(16)] + ["al%d" % i for i in range(3)] + ["ar%d" % i for i in range(3)])
PF, GF, KF, G15, K15, ND, SC, BI, BMIN, WL1, WL2, KLO = range(12)
TH, GAP, G16, VF, KC, KR = 12, 15, 21, 22, 28, 29


def tracker(g, T):
    queues = {"v": g.vector, "a": g.scalar, "p": g.tensor, "g": g, "s": g.sync}
    count, clock, order, recs, waited = {}, {}, {}, {}, {}
    known = {e: {} for e in queues}
    serial = [0]

    def wait(eng, key, n):
        if known[eng].get(key, 0) >= n:
            return
        queues[eng].wait_ge(T.sem[key], n)
        waited[key] = max(waited.get(key, 0), n)
        for k2, n2 in clock.get((key, n), {}).items():
            known[eng][k2] = max(known[eng].get(k2, 0), n2)
        known[eng][key] = n

    def settle(eng, reads, writes):
        need = {}
        for kind, accs in (("r", reads), ("w", writes)):
            for b, lo, hi in accs:
                ps = b in BANKS
                for rk, rlo, rhi, who, key, n in recs.get(b, ()):
                    over = rlo < hi and lo < rhi
                    if who == eng:
                        if eng == "p" or not over or rk == kind == "r":
                            continue
                    elif not ps and (not over or rk == kind == "r"):
                        continue
                    need[key] = max(need.get(key, 0), n)
        for key in sorted(need, key=lambda k: -order[(k, need[k])]):
            wait(eng, key, need[key])

    def note(who, key, n, reads, writes):
        serial[0] += 1
        order[(key, n)] = serial[0]
        for kind, accs in (("r", reads), ("w", writes)):
            for b, lo, hi in accs:
                recs.setdefault(b, []).append((kind, lo, hi, who, key, n))

    def emit(eng, fn, reads, writes, dma=None):
        settle(eng, reads, writes)
        key, step = (dma, 16) if dma else ("c" + eng, 1)
        n = count.get(key, 0) + step
        fn().then_inc(T.sem[key], step)
        count[key] = n
        clock[(key, n)] = dict(known[eng])
        note("dma " + dma if dma else eng, key, n, reads, writes)

    def remote(reads, key, n, fn):
        settle("g", reads, [])
        fn()
        count[key] = count.get(key, 0) + n
        note("net " + key, key, count[key], reads, [])

    def landing(key, n, writes):
        count[key] = n
        note("net " + key, key, n, [], writes)

    def finish():
        for key in sorted(count):
            if waited.get(key, 0) < count[key]:
                wait("s", key, count[key])

    return {"emit": emit, "remote": remote, "landing": landing, "finish": finish}


def rank_program(g, core, T, topo):
    rank = T.rank_of(core)
    if rank is None:
        return
    tr = tracker(g, T)
    emit = tr["emit"]
    nranks = len(T.cores)

    def S(name, lo, hi, step=1):
        if step == 1:
            return T[name][:, lo:hi], [(name, lo, hi)]
        return T[name][:, lo:hi:step], [(name, lo, hi)]

    def W(name, lo, hi, lname, l0, l1):
        return T[name][:, lo:hi].indirect(T[lname][:, l0:l1]), [(name, lo, hi), (lname, l0, l1)]

    def C(col):
        return S("cc", col, col + 1)

    def split(x):
        return (x[0], x[1]) if isinstance(x, tuple) else (x, [])

    def ts(out, in0, s1, s2, op0, op1=None):
        (a1, r1), (a2, r2) = split(s1), split(s2)
        if op1 is None:
            emit("v", lambda: g.vector.tensor_scalar(out[0], in0[0], a1, None, op0), in0[1] + r1, out[1])
        else:
            emit("v", lambda: g.vector.tensor_scalar(out[0], in0[0], a1, a2, op0, op1), in0[1] + r1 + r2, out[1])

    def tt(out, in0, in1, op):
        emit("v", lambda: g.vector.tensor_tensor(out[0], in0[0], in1[0], op), in0[1] + in1[1], out[1])

    def vcopy(out, in_):
        emit("v", lambda: g.vector.tensor_copy(out[0], in_[0]), in_[1], out[1])

    def vscatter(win, in_):
        emit("v", lambda: g.vector.tensor_copy(win[0], in_[0]), in_[1] + win[1][1:], win[1][:1])

    def vfill(out, c):
        emit("v", lambda: g.vector.memset(out[0], c), [], out[1])

    def scan(out, d0, d1, init, op0, op1):
        ai, ri = split(init)
        emit("v", lambda: g.vector.tensor_tensor_scan(out[0], d0[0], d1[0], ai, op0, op1), d0[1] + d1[1] + ri, out[1])

    def act(out, in_, func, bias=0.0, scale=1.0):
        (ab, rb), (asc, rs) = split(bias), split(scale)
        emit("a", lambda: g.scalar.activation(out[0], in_[0], func, bias=ab, scale=asc), in_[1] + rb + rs, out[1])

    def mms(items):
        def go():
            last = None
            for o, l, r, a, b in items:
                last = g.tensor.matmul(o[0], l[0], r[0], a, b)
            return last
        emit("p", go, sorted({a for i in items for a in i[1][1] + i[2][1]}), sorted({a for i in items for a in i[0][1]}))

    def iota(name, lo, hi, pattern, base, cm):
        if name == "ip":
            emit("g", lambda: g.iota(T[name][:, lo:hi], pattern, base, cm), [], [(name, lo, hi)])
        else:
            emit("g", lambda: g.iota(T[name][:, lo:hi], pattern, base, cm, allow_small_or_imprecise_dtypes=True), [], [(name, lo, hi)])

    def gfill(name, lo, hi, value):
        iota(name, lo, hi, [[0, hi - lo]], value, 0)

    def load(eng, sem, out, src):
        q = g.sync if eng == "s" else g.scalar
        emit(eng, lambda: q.dma_start(out[0], src), [], out[1], dma=sem)

    def win(name, k):
        return S(name, 15 - k, 143 - k)

    def wrap(out, lhs, name, lo, hi):
        mms([(out, win(lhs, k), S(name, lo + k, hi, 16), k == 0, k == 15) for k in range(16)])

    def tap(t, j):
        i = 3 * t + j
        return T.wbd[:, i, :], [("wbd", i, i + 1)]

    load("a", "dv", S("vb", 0, 3), T.v[:])
    for c in range(4):
        load("s", "dx%d" % c, S("big", 1024 * c, 1024 * c + 1024), T.x[:, 1024 * c:1024 * c + 1024])
    load("a", "dt", S("thi", 0, 3), T.th[:])
    load("a", "dg", S("gpi", 0, 3), T.gap[:])
    load("a", "dwt", (T.wb[:, :, :], [("wb", 0, 9)]), T.w[:])

    iota("ip", 0, 1, [[0, 1]], 0, 1)
    iota("jrow", 0, 144, [[1, 144]], 0, 0)
    iota("jg", 0, 128, [[1, 8], [0, 16]], 0, 0)
    iota("ir", 0, 256, [[16, 256]], 0, 1)
    iota("m16", 0, 16, [[16, 16]], 0, 0)
    iota("mrow", 0, 256, [[1, 256]], 0, 0)
    iota("g8", 0, 8, [[1, 8]], 0, 0)
    for t in range(3):
        gfill("rm%d" % t, 0, 16, 0)
    gfill("rm0", 288, 304, 0)
    gfill("dw0", 1024, CAP, 0)
    for t in range(3):
        if rank == 0:
            gfill("xc%d" % t, 0, HALO, 0)
        if rank == nranks - 1:
            gfill("xc%d" % t, XW, XW + HALO, 0)
    gfill("ones", 0, 512, 1)
    gfill("dw1", 0, CAP, 0)
    ts(S("gi", 0, 1), S("ip", 0, 1), 4, None, OP.logical_shift_right)
    ts(S("ki", 0, 1), S("ip", 0, 1), 15, None, OP.bitwise_and)
    vcopy(C(PF), S("ip", 0, 1))
    vcopy(C(GF), S("gi", 0, 1))
    vcopy(C(KF), S("ki", 0, 1))
    ts(C(G15), C(GF), 16.0, 15.0, OP.mult, OP.add)
    ts(C(K15), C(KF), 15.0, None, OP.is_equal)
    ts(S("e", 0, 144), S("jrow", 0, 144), C(G15), None, OP.is_equal)
    ts(S("sv0", 0, 144), S("e", 0, 144), S("vb", 0, 1), None, OP.mult)
    for col, sc, bi in ((ND, 1.0, -1.0), (SC, 2.0, -1.0), (BI, -1.0, 1.0), (BMIN, 255.0, 1.0), (WL1, 15.0, 1.0), (WL2, 17.0, -1.0)):
        act(C(col), C(K15), AF.Identity, bias=bi, scale=sc)
    act(C(G16), C(GF), AF.Copy, scale=-16.0)
    act(C(KLO), C(KF), AF.Copy, scale=-1.0 / 8192)
    ts(S("bd", 0, 128), S("jg", 0, 128), C(GF), None, OP.is_equal)
    ts(S("ltf", 0, 128), S("jrow", 0, 128), C(PF), None, OP.is_ge)
    ts(S("idn", 0, 128), S("jrow", 0, 128), C(PF), None, OP.is_equal)
    tt(S("ltf", 0, 128), S("ltf", 0, 128), S("bd", 0, 128), OP.mult)
    ts(S("s15", 0, 128), S("idn", 0, 128), C(K15), None, OP.mult)
    tt(S("lt", 0, 128), S("ltf", 0, 128), S("e", 0, 128), OP.subtract)
    vcopy(S("cc", TH, TH + 3), S("thi", 0, 3))
    vfill(S("dw0", 0, 1024), 0.0)
    vcopy(S("cc", GAP, GAP + 3), S("gpi", 0, 3))
    vcopy(S("cc", VF, VF + 3), S("vb", 0, 3))
    ts(S("iw", 0, 256), S("ir", 0, 256), C(G16), None, OP.add)
    ts(S("chi", 0, 16), S("m16", 0, 16), 2048.0, -1.0 / 8192, OP.add, OP.mult)
    ts(S("clo", 0, 16), S("m16", 0, 16), 0.0, C(KLO), OP.mult, OP.add)
    for lo in (0, 1024):
        act(S("dc", lo, lo + 1024), S("big", 0, 1024), AF.Identity, bias=C(ND), scale=0.0)
    for t in (1, 2):
        act(S("sv%d" % t, 0, 144), S("e", 0, 144), AF.Copy, scale=C(VF + t))
    ts(S("gm", 0, 8), S("g8", 0, 8), C(GF), 0.125, OP.is_equal, OP.mult)
    act(S("iwd0", 0, 128), S("iw", 0, 128), AF.Identity, bias=C(GAP))
    act(S("qk", 0, 4), S("iw", 0, 4), AF.Identity, bias=-64.0)
    act(S("el1", 0, 144), S("e", 0, 144), AF.Copy, scale=C(WL1))
    act(S("el2", 0, 144), S("e", 0, 144), AF.Copy, scale=C(WL2))
    base = [4096 - 1 - 8192, 2048 - 1 - 8192]

    def tap_matrices(first, last):
        for i in range(first, last):
            emit("a", lambda: g.scalar.activation(T.wbd[:, :, 16 * i:16 * i + 16], T.wb[:, :, :], AF.Copy, scale=T.gm[:, i:i + 1]),
                 [("wb", 0, 9), ("gm", i, i + 1)], [("wbd", 0, 9)] if i == 7 else [])

    def later_constants():
        for i, n in ((0, 256), (1, 128)):
            act(S("own%d" % i, 0, n), S("iw", 0, n), AF.Identity, bias=float(-base[i]))
        for t in (1, 2):
            act(S("iwd%d" % t, 0, 128), S("iw", 0, 128), AF.Identity, bias=C(GAP + t))
            act(C(TH + t), S("b3", 300 + t, 301 + t), AF.Identity, bias=C(TH + t), scale=OFS)

    def shift_lists(t):
        ts(S("lst%d" % t, 0, 4), S("iw", 0, 4), C(GAP + t), 64.0, OP.subtract, OP.add)
        ts(S("lb%d" % t, 4, 128), S("iw", 4, 128), C(GAP + t), None, OP.subtract)

    def slots_a(t):
        n = 128 if t else 256
        tt(S("st", 0, n), S("own%d" % (t > 0), 0, n), S("b3", 16, 16 + n), OP.max)

    def slots_b(t):
        n = 128 if t else 256
        ts(S("slot%d" % t, 0, n), S("st", 0, n), float(base[t > 0]), None, OP.add)

    zoff = [Z1, Z2, Z3]

    def send(t):
        fl, x = "fl%d" % t, "xc%d" % t
        out = []
        if rank > 0:
            out.append((rank - 1, S(fl, 0, HALO), T[x][:, XW:XW + HALO], "ar%d" % t))
        if rank < nranks - 1:
            out.append((rank + 1, S(fl, HALO, 2 * HALO), T[x][:, 0:HALO], "al%d" % t))
        reads = [a for o in out for a in o[1][1]]
        if len(out) == 1:
            dst = T.cores[out[0][0]]
            a = topo.addr(dst)
            tr["remote"](reads, "sent", len(topo.engines(core, dst)), lambda: g.remote_dma(
                out_ap=out[0][2], in_ap=out[0][1][0], remote_sem=T.sem[out[0][3]], local_sem=T.sem.sent,
                pid=a[1], routing_id=a[0], dma_engine_mask=topo.mask(core, dst)))
            return
        trs, used = [], 0
        for i, o in enumerate(out):
            dst = T.cores[o[0]]
            a = topo.addr(dst)
            en = topo.engines(core, dst)
            half = len(en) // 2
            mine = en[:half] if i == 0 else en[half:]
            used += len(mine)
            trs.append(RemoteDMATransfer(dst_ids=[DstId(rid=a[0], pnc=a[1])], dma_engine_mask=sum(1 << k for k in mine),
                                         remote_sem=T.sem[o[3]], src=o[1][0], dst=o[2]))
        tr["remote"](reads, "sent", used, lambda: g.remote_dma_fused(trs, local_sem=T.sem.sent))

    for t in range(3):
        for peer, key, lo in ((rank - 1, "al%d" % t, 0), (rank + 1, "ar%d" % t, XW)):
            if 0 <= peer < nranks:
                en = len(topo.engines(T.cores[peer], core))
                tr["landing"](key, en if peer in (0, nranks - 1) else en // 2, [("xc%d" % t, lo, lo + HALO)])

    def scores(t, half):
        ob = S("b0", 0, 64) if half == 0 else S("b2", 0, 64)
        c0, s0 = 64 * half, zoff[t - 1] + 1024 * half
        mms([(ob, S("idn", 0, 128), S("pen%d" % t, c0, c0 + 64), True, False)]
            + [(ob, win("sv%d" % t, k), S("big", s0 + k, s0 + 1024, 16), False, k == 15) for k in range(16)])

    def back(eng, level, lo, hi):
        src, top = ((0, V1), (Z1, V2), (Z2, Z3))[level]
        i = W("big", src, top + min(hi, CAP), "slot%d" % level, lo // 16, hi // 16)
        o = S("yb", lo, hi) if level == 0 else S("big", (0, V1, V2)[level] + lo, (0, V1, V2)[level] + hi)
        if eng == "a":
            act(o, i, AF.Copy) if level != 1 else act(o, i, AF.Identity, bias=-OFS)
        elif level != 1:
            vcopy(o, i)
        else:
            ts(o, i, -OFS, None, OP.add)

    def store(lo, hi):
        emit("s", lambda: g.sync.dma_start(T.y[:, lo:hi], T.yb[:, lo:hi]), [("yb", lo, hi)], [], dma="dy%d" % (lo // 256))

    for t in range(3):
        rm, dw, xc, lst, fl, sv = ["%s%d" % (n, t) for n in ("rm", "dw", "xc", "lst", "fl", "sv")]
        space = (0, 4096) if t == 0 else (zoff[t - 1], zoff[t - 1] + CAP)
        z = zoff[t]
        P0 = (16, 304) if t == 0 else (16,)
        last = len(P0) - 1

        def mark(p):
            m0, r0, c0, w0, o = P0[p], P0[p] + 128, 128 * p, 8 * p, 32 * p
            mms([(S("b1", c0, c0 + 128), S("lt", 0, 128), S(rm, m0, r0), True, False),
                 (S("b1", c0, c0 + 128), S("s15", 0, 128), S("mrow", c0, c0 + 128), False, True)])
            scan(S(rm, r0, r0 + 129), S(rm, m0 - 1, r0), S(rm, m0 - 1, r0), S(rm, P0[0] + 256, P0[0] + 257) if p else 0.0, OP.add, OP.max)
            act(S("dsb", c0, c0 + 128), S("b1", c0, c0 + 128), AF.Copy)
            if p == last:
                mms([(S("b3", 0, 1), S("bd", 0, 128), S(rm, r0 + 128, r0 + 129), True, True)])
            b2, b2m = S("b2", o, o + 16), S("b2", o, o + 8)
            rhs = [(win("e", k), S(rm, m0 + k, m0 + 256, 16)) for k in range(16)]
            mms([(b2, rhs[0][0], rhs[0][1], True, False),
                 (b2m, S("idn", 0, 128), S("chi", w0, w0 + 8), False, False), (b2m, S("idn", 0, 128), S("clo", w0, w0 + 8), False, False)]
                + [(b2, rhs[k][0], rhs[k][1], False, k == 15) for k in range(1, 16)])

        def offsets(p, fill1=None, fill2=None):
            w0, o = 8 * p, 32 * p
            ts(S("of1", w0, w0 + 8), S("b2", o, o + 8), -8192.0, None, OP.mult)
            if fill1:
                fill1()
            tt(S("of2", w0, w0 + 8), S("of1", w0, w0 + 8), S("b2", o + 8, o + 16), OP.max)
            if fill2:
                fill2()
            vcopy(S("off%d" % t, w0, w0 + 8), S("of2", w0, w0 + 8))

        def scatter(p):
            vscatter(W(dw, 0, DWW, "off%d" % t, 8 * p, 8 * p + 8), S("dsb", 128 * p, 128 * p + 128))

        def pick(eng, out, lname, l0, l1):
            i = W("big", *space, lname, l0, l1)
            if eng == "a":
                act(out, i, AF.Copy) if t == 0 else act(out, i, AF.Identity, bias=-OFS)
            else:
                vcopy(out, i) if t == 0 else ts(out, i, -OFS, None, OP.add)

        def left(eng, lo, hi):
            o, i = S("gb", lo, hi), W(xc, HALO, HALO + hi, "lb%d" % t, lo // 16, hi // 16)
            act(o, i, AF.Copy) if eng == "a" else vcopy(o, i)

        def right(eng, lo, hi):
            o, i = S("gc", lo, hi), W(xc, HALO, XW + HALO, "lc%d" % t, lo // 16, hi // 16)
            act(o, i, AF.Copy) if eng == "a" else vcopy(o, i)

        def bank(c):
            return S(("b4", "b5", "b6", "b7", "b1")[c], 0, PARTS[c][1] - PARTS[c][0])

        def offset(c):
            mms([(bank(c), S("idb", 0, 128), S("ones", 0, PARTS[c][1] - PARTS[c][0]), True, False)])

        def mix(c, j):
            lo, hi = PARTS[c]
            mms([(bank(c), tap(t, j), S(*((xc, HALO + lo, HALO + hi), ("gb", lo, hi), ("gc", lo, hi))[j]), False, j == 2)])

        def near(c):
            lo, hi = PARTS[c]
            ts(S("big", z + lo, z + hi), bank(c), OFS - 15.0, OFS + 15.0, OP.max, OP.min)

        if t == 0:
            for c in range(4):
                wrap(S("b0" if c < 2 else "b3", 64 * (c % 2), 64 * (c % 2) + 64), sv, "big", 1024 * c, 1024 * c + 1024)
                if c == 1:
                    ts(S(rm, 16, 144), S("b0", 0, 128), C(TH), None, OP.is_ge)
                if c == 2:
                    tap_matrices(0, 2)
                    mark(0)
            shift_lists(0)
            for name, c in (("idk", 8192.0), ("idb", OFS)):
                ts(S(name, 0, 128), S("idn", 0, 128), c, None, OP.mult)
            offsets(0)
            ts(S(rm, 304, 432), S("b3", 0, 128), C(TH), None, OP.is_ge)
        else:
            scores(t, 1)
            shift_lists(t)
            slots_a(t - 1)
            ts(S(rm, 16, 80), S("b0", 0, 64), C(TH + t), None, OP.is_ge)
            ts(S(rm, 80, 144), S("b2", 0, 64), C(TH + t), None, OP.is_ge)
        mark(last)
        if t == 0:
            scatter(0)
        else:
            slots_b(t - 1)
        act(C(KR), S("b3", 0, 1), AF.Copy)
        act(C(KC), S("b3", 0, 1), AF.Copy, bias=float(XW - HALO), scale=-1.0)
        lcsel = S("b0", 256, 384)
        offsets(last, lambda: ts(lcsel, S("iwd%d" % t, 0, 128), C(KR), C(KC), OP.is_ge, OP.mult),
                lambda: ts(S(lst, 4, 8), S("qk", 0, 4), C(KR), None, OP.add))
        scatter(last)
        for p in range(last + 1):
            cum, m0 = S("b3", 16 + 128 * p, 144 + 128 * p), P0[p]
            mms([(cum, S("bd", 0, 128), S(rm, m0 + 128, m0 + 256), True, False), (cum, S("ltf", 0, 128), S(rm, m0, m0 + 128), False, False),
                 (cum, S("idk", 0, 128), S(rm, m0, m0 + 128), False, True)])
        if t == 0:
            tap_matrices(2, 8)
            mms([(S("b3", 300, 303), S("bd", 0, 128), S("vb", 0, 3), True, True)])
        u0 = 0.0
        for lo, hi in ((0, 512), (512, 1024), (1024, 2048)):
            scan(S("u", lo, hi), S("dc", lo, hi), S(dw, lo, hi), u0, OP.add, OP.max)
            if lo < 1024:
                act(S("cb", lo, hi), S("u", lo, hi), AF.Relu, bias=C(BI), scale=C(SC))
            if lo == 0:
                tt(S("lcf", 0, 128), S("iwd%d" % t, 0, 128), lcsel, OP.add)
            if lo == 512:
                ts(S("cf", 0, 64), S("u", 0, 64), C(BMIN), None, OP.min)
            if lo == 1024:
                ts(S("lc%d" % t, 0, 128), S("lcf", 0, 128), float(CAP + HALO - 1), None, OP.min)
            u0 = S("u", hi - 1, hi)
        ts(S("cf", 64, 128), W("u", 0, CAP, lst, 4, 8), C(BMIN), None, OP.min)
        for c in range(3):
            offset(c)
        wrap(S("b1", 0, 32), "el1", "cb", 0, 512)
        wrap(S("b2", 0, 8), "el2", "cf", 0, 128)
        vcopy(S("la%d" % t, 0, 32), S("b1", 0, 32))
        pick("a", S(xc, 64, 576), "la%d" % t, 0, 32)
        ts(S("cb", 1024, 2048), S("u", 1024, 2048), C(BMIN), None, OP.min)
        ts(S("fll%d" % t, 0, 8), S("b2", 0, 8), 15.0, None, OP.add)
        pick("v", S(fl, 0, 128), "fll%d" % t, 0, 8)
        send(t)
        wrap(S("b1", 0, 32), "el1", "cb", 512, 1024)
        wrap(S("b0", 0, 64), "el2", "cb", 1024, 2048)
        vcopy(S("lm%d" % t, 0, 32), S("b1", 0, 32))
        pick("a", S(xc, 576, 1088), "lm%d" % t, 0, 32)
        ts(S("ll%d" % t, 0, 64), S("b0", 0, 64), 15.0, None, OP.add)
        pick("v", S(xc, 1088, 64 + CUT), "ll%d" % t, 0, CUT // 16 - 64)
        pick("a", S(xc, 64 + CUT, 2112), "ll%d" % t, CUT // 16 - 64, 64)
        offset(3)
        offset(4)
        left("a", 64, 512)
        left("v", 1024, 1536)
        left("a", 512, 1024)
        left("v", 1536, 2048)
        for c in range(5):
            mix(c, 0)
        vcopy(S("gb", 0, 64), W(xc, 0, HALO + 64, lst, 0, 4))
        right("a", 0, 512)
        for c in (2, 1, 3, 4, 0):
            mix(c, 1)
        right("v", 1536, 1920)
        mix(0, 2)
        right("a", 512, 1024)
        mix(3, 2)
        right("a", 1024, 1536)
        mix(1, 2)
        if t < 2:
            ts(S("pen%d" % (t + 1), 0, 128), S("iw", 0, 128), C(KR), -32768.0, OP.is_ge, OP.mult)
        else:
            slots_a(2)
        right("a", 1920, 2048)
        if t == 0:
            later_constants()
        mix(2, 2)
        mix(4, 2)
        if t == 2:
            slots_b(2)
        near(0)
        if t == 2:
            back("a", 2, 0, 512)
        near(3)
        near(1)
        if t == 2:
            back("a", 1, 0, 512)
        if t < 2:
            scores(t + 1, 0)
        near(2)
        near(4)
        if t == 0:
            gfill("dw2", 0, CAP, 0)

    for level, c in ((2, 1), (0, 0), (1, 1), (2, 2), (0, 1), (1, 2), (2, 3), (0, 2), (1, 3), (0, 3), (0, 4), (0, 5), (0, 6), (0, 7)):
        for lo, hi in ((512 * c, 512 * c + 512),) if (level, c) != (0, 7) else ((3584, 3840), (3840, 4096)):
            mid = (lo + hi) // 2
            back("a", level, lo, mid)
            back("v", level, mid, hi)
            if level == 0:
                store(lo, hi)
    tr["finish"]()
